import numpy as np
import ml_dtypes


def mxq(x, axis, fmt="e4m3"):
    dtype, down = {"e4m3": (ml_dtypes.float8_e4m3fn, 7), "e5m2": (ml_dtypes.float8_e5m2, 14)}[fmt]
    v = np.moveaxis(np.asarray(x, np.float32).astype(ml_dtypes.bfloat16).astype(np.float64), axis, -1)
    blocks = v.reshape(v.shape[:-1] + (-1, 32))
    amax = np.abs(blocks).max(-1, keepdims=True)
    byte = np.maximum(np.where(amax > 0, np.frexp(amax)[1] - 1 + 127, 0) - down, 1)
    scale = np.exp2(byte - 127.0)
    codes = (blocks / scale).astype(np.float32).astype(dtype).astype(np.float64)
    return np.moveaxis((codes * scale).reshape(v.shape), -1, axis)


WIDE = False


def mx_kscale(k):
    if not WIDE:
        return np.ones(k)
    levels = np.array([24, -24, 12, -12, 0])
    if k % 512:
        return np.exp2(np.random.permutation(np.resize(levels, k // 32))).repeat(32)
    a = np.empty((k // 512, 16))
    for p in range(k // 512):
        a[p, :8] = np.random.permutation(np.resize(levels, 8))
        for g in range(8):
            far = levels[np.abs(levels - a[p, g]) >= 10]
            a[p, g + 8] = far[np.random.randint(len(far))]
    return np.exp2(a.ravel()).repeat(32)


def f64(x):
    return np.asarray(x).astype(np.float64)


def striped(idx):
    return np.tile(idx.reshape(-1, 16).T, (8, 1)).astype(np.uint16)


def unstriped(offs):
    return offs[:16].T.reshape(-1).astype(np.int64)


E2M1 = np.array([0.0, 0.5, 1.0, 1.5, 2.0, 3.0, 4.0, 6.0, -0.0, -0.5, -1.0, -1.5, -2.0, -3.0, -4.0, -6.0])


def pack_weight(w, fmt):
    k, n = w.shape
    w = f64(np.asarray(w, np.float32).astype(ml_dtypes.bfloat16)).reshape(k // 32, 32, n)
    amax = np.abs(w).max(1)
    if fmt == "e4m3":
        byte = np.frexp(amax)[1] - 1 + 127 - 7
    else:
        mant, ex = np.frexp(amax / 6.0)
        byte = np.where(mant > 0.5, ex, ex - 1) + 127
    byte = np.clip(np.where(amax > 0, byte, 1), 1, 254)
    scaled = (w * np.exp2(127.0 - byte)[:, None, :]).reshape(k, n).astype(np.float32)
    by_word = np.ascontiguousarray(scaled.reshape(k // 512, 128, 4, n).transpose(0, 1, 3, 2))
    if fmt == "e4m3":
        words = by_word.astype(ml_dtypes.float8_e4m3fn).view(np.uint8)
    else:
        c = by_word.astype(ml_dtypes.float4_e2m1fn).view(np.uint8) & 0xF
        words = (c[..., 0::2] | (c[..., 1::2] << 4)).reshape(k // 512, 128, 2 * n)
    return np.ascontiguousarray(words), np.ascontiguousarray(byte.astype(np.uint8).reshape(k // 512, 16, n))


def unpack_weight(words, scales, fmt):
    g, _, n = scales.shape
    words = np.ascontiguousarray(words).reshape(g, 128, n, -1)
    if fmt == "e4m3":
        vals = words.view(ml_dtypes.float8_e4m3fn).astype(np.float64)
    else:
        nib = np.empty((g, 128, n, 4), np.uint8)
        nib[..., 0::2] = words & 0xF
        nib[..., 1::2] = words >> 4
        vals = E2M1[nib]
    vals = vals * np.repeat(np.exp2(scales.astype(np.float64) - 127.0), 8, axis=1)[..., None]
    return vals.transpose(0, 1, 3, 2).reshape(g * 512, n)


def silu(f):
    return f / (1.0 + np.exp(-np.maximum(f, -700.0)))


K, R, N, T, J = 1024, 512, 512, 2048, 1024


def setup_inputs():
    n = np.random.standard_normal
    s = mx_kscale(K)[:, None]
    u = mx_kscale(R)[:, None]
    p_tab = pack_weight(n((K, T)) * s, "e4m3")
    p_wu = pack_weight(n((K, R)) / np.sqrt(K) / s, "e4m3")
    p_wd = pack_weight(n((R, N)) / np.sqrt(R) / u, "e2m1")
    return {
        "tab_words": p_tab[0],
        "tab_scales": p_tab[1],
        "wu_words": p_wu[0],
        "wu_scales": p_wu[1],
        "sm": (np.random.uniform(0.5, 2.0, R) * u[:, 0]).astype(np.float32),
        "wd_words": p_wd[0],
        "wd_scales": p_wd[1],
        "wgo": np.tile(np.random.uniform(0.5, 2.0, J), (128, 1)).astype(np.float32),
        "offs": striped(np.random.permutation(T)[:J]),
    }


def reference(tab_words, tab_scales, wu_words, wu_scales, sm, wd_words, wd_scales, wgo, offs):
    idx = unstriped(offs)
    tab_ = unpack_weight(tab_words, tab_scales, "e4m3")[:, idx]
    wu_ = unpack_weight(wu_words, wu_scales, "e4m3")
    a = wu_.T @ tab_
    h = f64(sm)[:, None] * silu(a)
    h_ = mxq(h, 0, "e4m3")
    wd_ = unpack_weight(wd_words, wd_scales, "e2m1")
    y = wd_.T @ h_
    out = np.zeros((N, T))
    out[:, idx] = f64(wgo)[0] * (y)
    return out

@@ -1,0 +1,194 @@
+from contextlib import ExitStack
+
+import concourse.mybir as mybir
+
+K, R, N, T, J = 1024, 512, 512, 2048, 1024
+FLOPS = 2 * K * R * J + 2 * R * N * J
+
+F32 = mybir.dt.float32
+BF16 = mybir.dt.bfloat16
+I32 = mybir.dt.int32
+U32 = mybir.dt.uint32
+U16 = mybir.dt.uint16
+U8 = mybir.dt.uint8
+FP8X4 = mybir.dt.float8_e4m3fn_x4
+FP4X4 = mybir.dt.float4_e2m1fn_x4
+ACT = mybir.ActivationFunctionType
+MULT = mybir.AluOpType.mult
+
+P = 128
+PACK = 4
+PASSES = K // (P * PACK)
+CHUNK = 256
+CHUNKS = J // CHUNK
+ROW_TILES = N // P
+LIST_ROWS = 16
+
+
+def tile_list_modp_silu_none_kernel(
+    tc, tab_words, tab_scales, wu_words, wu_scales, sm, wd_words, wd_scales, wgo, offs, out
+):
+    nc = tc.nc
+    with ExitStack() as ctx:
+        keep = ctx.enter_context(tc.tile_pool(name="keep", bufs=1))
+        ring = ctx.enter_context(tc.tile_pool(name="ring", bufs=2))
+        psum = ctx.enter_context(tc.psum_pool(name="psum", bufs=1))
+
+        offsets = keep.tile([P, J // LIST_ROWS], U16, name="offsets")
+        tab_w = [keep.tile([P, T], I32, name="tab_w%d" % a, align_bytes=64) for a in range(PASSES)]
+        tab_s = keep.tile([P, T // 4], I32, name="tab_s", align_bytes=64)
+        wu_raw = keep.tile([P, PASSES, R], I32, name="wu_raw", tag="wu_then_wgo", align_bytes=64)
+        wu_s_raw = keep.tile([P, R // 4], I32, name="wu_s_raw", align_bytes=64)
+        wu_w = keep.tile([P, PASSES, R], I32, name="wu_w", align_bytes=64)
+        wu_s = keep.tile([P, R], U8, name="wu_s", align_bytes=64)
+        wd_w = keep.tile([P, N // 2], I32, name="wd_w", align_bytes=64)
+        wd_s = keep.tile([P, N // 4], I32, name="wd_s", align_bytes=64)
+        sm_t = keep.tile([P, PACK], F32, name="sm_t")
+        v_s = keep.tile([P, J], U8, name="v_s", align_bytes=64)
+        h_w = keep.tile([P, J], U32, name="h_w", align_bytes=64)
+        h_s = keep.tile([P, J], U8, name="h_s", align_bytes=64)
+        placed = [keep.tile([P, T], F32, name="placed%d" % n) for n in range(ROW_TILES)]
+        warm = keep.tile([P, 1], F32, name="warm")
+        warm_out = keep.tile([P, 1], F32, name="warm_out")
+
+        nc.gpsimd.memset(tab_s[:], 0)
+        nc.vector.memset(wu_s_raw[:], 0)
+        nc.gpsimd.memset(wd_s[:], 0)
+        nc.sync.dma_start(offsets[:], offs)
+        nc.sync.dma_start(out=wu_raw[:], in_=wu_words.rearrange("a p r i -> p a (r i)").bitcast(I32))
+        for q in range(4):
+            nc.scalar.dma_start(
+                out=tab_s[32 * q : 32 * q + 4 * PASSES, :], in_=tab_scales[:, 4 * q : 4 * q + 4, :].bitcast(I32)
+            )
+        for a in range(PASSES):
+            nc.sync.dma_start(out=tab_w[a][:], in_=tab_words[a].rearrange("p t i -> p (t i)").bitcast(I32))
+        for q in range(4):
+            nc.scalar.dma_start(
+                out=wu_s_raw[32 * q : 32 * q + 4 * PASSES, :], in_=wu_scales[:, 4 * q : 4 * q + 4, :].bitcast(I32)
+            )
+        nc.vector.memset(warm[:], 0.0)
+        nc.scalar.activation(out=warm_out[:], in_=warm[:], func=ACT.Silu)
+        nc.gpsimd.dma_start(out=sm_t[:], in_=sm.rearrange("(p t) -> p t", t=PACK))
+        for q in range(4):
+            nc.gpsimd.dma_start(out=wd_s[32 * q : 32 * q + 4, :], in_=wd_scales[0, 4 * q : 4 * q + 4, :].bitcast(I32))
+
+        def cols(c, count=1):
+            return slice(c * CHUNK, (c + count) * CHUNK)
+
+        def listed(c, count=1):
+            return offsets[:, c * CHUNK // LIST_ROWS : (c + count) * CHUNK // LIST_ROWS]
+
+        def gather_scales(c, count=1):
+            nc.vector.tensor_copy(v_s[:, cols(c, count)], tab_s[:].bitcast(U8).indirect(listed(c, count)))
+
+        def gather_words(c, count=1):
+            words = []
+            for a in range(PASSES):
+                v_w = ring.tile([P, count * CHUNK], U32, name="v_w%d" % a, align_bytes=64)
+                nc.vector.tensor_copy(v_w[:], tab_w[a][:].bitcast(U32).indirect(listed(c, count)))
+                words.append(v_w)
+            return words
+
+        def up(words, c, count=1):
+            width = count * CHUNK
+            act = ring.tile([P, PACK, width], F32, name="act")
+            banks = [psum.tile([P, width], F32, name="up%d" % t) for t in range(PACK)]
+            for a in range(PASSES):
+                for t in range(PACK):
+                    nc.tensor.matmul_mx(
+                        out=banks[t][:],
+                        lhsT=wu_w[:, a, t * P : (t + 1) * P].bitcast(FP8X4),
+                        lhsT_scale=wu_s[4 * a :, t * P : (t + 1) * P],
+                        rhs=words[a][:].bitcast(FP8X4),
+                        rhs_scale=v_s[4 * a :, cols(c, count)],
+                        start=(a == 0),
+                        stop=(a == PASSES - 1),
+                    )
+            for t in range(PACK):
+                nc.scalar.activation(out=act[:, t, :], in_=banks[t][:], func=ACT.Silu)
+            return act
+
+        def smooth_on_vector(act):
+            width = act.shape[2]
+            h = ring.tile([P, width, PACK], BF16, name="h", align_bytes=64)
+            nc.vector.tensor_tensor(
+                h[:], act[:].rearrange("p t j -> p j t"), sm_t[:].unsqueeze(1).to_broadcast([P, width, PACK]), MULT
+            )
+            return h
+
+        def smooth_on_scalar(act, tag):
+            width = act.shape[2]
+            planes = keep.tile([P, PACK, width], BF16, name="planes", tag=tag)
+            h = ring.tile([P, width, PACK], BF16, name="h", align_bytes=64)
+            for t in range(PACK):
+                nc.scalar.activation(out=planes[:, t, :], in_=act[:, t, :], func=ACT.Copy, scale=sm_t[:, t : t + 1])
+            nc.scalar.copy(out=h[:], in_=planes[:].rearrange("p t j -> p j t"))
+            return h
+
+        def quantize(c, h, count=1):
+            nc.vector.quantize_mx(
+                out=h_w[:, cols(c, count)].bitcast(FP8X4),
+                scales=h_s[:, cols(c, count)],
+                in_=h[:].rearrange("p j t -> p (j t)"),
+            )
+
+        def down(slot, n0, tiles, c, count, tag):
+            bank = psum.tile([P, tiles, count * CHUNK], F32, name="down%d" % slot)
+            for n in range(n0, n0 + tiles):
+                nc.tensor.matmul_mx(
+                    out=bank[:, n - n0, :],
+                    lhsT=wd_w[:, n * P // 2 : (n + 1) * P // 2].bitcast(U8).bitcast(FP4X4),
+                    lhsT_scale=wd_s[:].bitcast(U8)[:, n * P : (n + 1) * P],
+                    rhs=h_w[:, cols(c, count)].bitcast(FP8X4),
+                    rhs_scale=h_s[:, cols(c, count)],
+                    start=True,
+                    stop=True,
+                )
+            y = keep.tile([P, tiles, count * CHUNK], F32, name="y", tag=tag)
+            nc.scalar.copy(out=y[:], in_=bank[:])
+            for n in range(n0, n0 + tiles):
+                place(n, y[:, n - n0, :], c, count)
+
+        def place(n, y, c, count):
+            nc.vector.tensor_tensor(
+                placed[n][:].indirect(listed(c, count)), y, wgo_t[:, cols(c, count)], MULT
+            )
+
+        nc.vector.tensor_copy(
+            out=wu_w[:].rearrange("p a (t m) -> p a m t", t=PACK), in_=wu_raw[:].rearrange("p a (m t) -> p a m t", t=PACK)
+        )
+        wgo_t = keep.tile([P, J], F32, name="wgo_t", tag="wu_then_wgo", align_bytes=64)
+        nc.sync.dma_start(out=wgo_t[:], in_=wgo)
+        nc.vector.tensor_copy(
+            out=wu_s[:].rearrange("p (t m) -> p m t", t=PACK),
+            in_=wu_s_raw[:].bitcast(U8).rearrange("p (m t) -> p m t", t=PACK),
+        )
+
+        for c in range(CHUNKS):
+            gather_scales(c)
+        words0 = gather_words(0)
+        words1 = gather_words(1)
+
+        for n in range(2):
+            for c0 in range(0, T, 1024):
+                nc.vector.memset(placed[n][:, c0 : c0 + 1024], 0.0)
+        for c0 in range(0, T, 512):
+            nc.gpsimd.memset(placed[2][:, c0 : c0 + 512], 0.0)
+        nc.gpsimd.dma_start(out=wd_w[:], in_=wd_words[0].bitcast(I32))
+        for c0 in range(0, T, 512):
+            nc.gpsimd.memset(placed[3][:, c0 : c0 + 512], 0.0)
+
+        act = up(words0, 0)
+        words2 = gather_words(2, 2)
+        quantize(0, smooth_on_vector(act))
+        down(0, 0, 2, 0, 1, "y_a")
+        quantize(1, smooth_on_scalar(up(words1, 1), "stage1"))
+        down(1, 2, 2, 0, 1, "stage1")
+        act = up(words2, 2, 2)
+        down(2, 0, 2, 1, 1, "y_b")
+        down(3, 2, 1, 1, 1, "y_c")
+        quantize(2, smooth_on_scalar(act, "stage2"), 2)
+        down(0, 3, 1, 1, 1, "stage2")
+        for n in range(ROW_TILES):
+            down((n + 1) % 4, n, 1, 2, 2, "y%d" % n)
+            nc.sync.dma_start(out=out[n * P : (n + 1) * P, :], in_=placed[n][:])

@@ -35,7 +35,6 @@ def tile_list_modp_silu_none_kernel(
         psum = ctx.enter_context(tc.psum_pool(name="psum", bufs=1))
 
         offsets = keep.tile([P, J // LIST_ROWS], U16, name="offsets")
-        tab_w = [keep.tile([P, T], I32, name="tab_w%d" % a, align_bytes=64) for a in range(PASSES)]
         tab_s = keep.tile([P, T // 4], I32, name="tab_s", align_bytes=64)
         wu_raw = keep.tile([P, PASSES, R], I32, name="wu_raw", tag="wu_then_wgo", align_bytes=64)
         wu_s_raw = keep.tile([P, R // 4], I32, name="wu_s_raw", align_bytes=64)
@@ -48,29 +47,32 @@ def tile_list_modp_silu_none_kernel(
         h_w = keep.tile([P, J], U32, name="h_w", align_bytes=64)
         h_s = keep.tile([P, J], U8, name="h_s", align_bytes=64)
         placed = [keep.tile([P, T], F32, name="placed%d" % n) for n in range(ROW_TILES)]
-        warm = keep.tile([P, 1], F32, name="warm")
-        warm_out = keep.tile([P, 1], F32, name="warm_out")
+        warm = keep.tile([P, 1], F32, name="warm", tag="tab_w0", align_bytes=64)
+        warm_out = keep.tile([P, 1], F32, name="warm_out", tag="tab_w1", align_bytes=64)
+        v_w = [keep.tile([P, J], U32, name="v_w%d" % a, align_bytes=64) for a in range(PASSES)]
 
         nc.gpsimd.memset(tab_s[:], 0)
+        nc.vector.memset(warm[:], 0.0)
         nc.vector.memset(wu_s_raw[:], 0)
-        nc.gpsimd.memset(wd_s[:], 0)
+        nc.scalar.activation(out=warm_out[:], in_=warm[:], func=ACT.Silu)
+        tab_w = [keep.tile([P, T], I32, name="tab_w%d" % a, align_bytes=64) for a in range(PASSES)]
         nc.sync.dma_start(offsets[:], offs)
         nc.sync.dma_start(out=wu_raw[:], in_=wu_words.rearrange("a p r i -> p a (r i)").bitcast(I32))
         for q in range(4):
-            nc.scalar.dma_start(
+            nc.sync.dma_start(
                 out=tab_s[32 * q : 32 * q + 4 * PASSES, :], in_=tab_scales[:, 4 * q : 4 * q + 4, :].bitcast(I32)
             )
-        for a in range(PASSES):
-            nc.sync.dma_start(out=tab_w[a][:], in_=tab_words[a].rearrange("p t i -> p (t i)").bitcast(I32))
+        nc.sync.dma_start(out=tab_w[0][:], in_=tab_words[0].rearrange("p t i -> p (t i)").bitcast(I32))
         for q in range(4):
-            nc.scalar.dma_start(
+            nc.sync.dma_start(
                 out=wu_s_raw[32 * q : 32 * q + 4 * PASSES, :], in_=wu_scales[:, 4 * q : 4 * q + 4, :].bitcast(I32)
             )
-        nc.vector.memset(warm[:], 0.0)
-        nc.scalar.activation(out=warm_out[:], in_=warm[:], func=ACT.Silu)
+        nc.sync.dma_start(out=tab_w[1][:], in_=tab_words[1].rearrange("p t i -> p (t i)").bitcast(I32))
         nc.gpsimd.dma_start(out=sm_t[:], in_=sm.rearrange("(p t) -> p t", t=PACK))
+        nc.gpsimd.memset(wd_s[:], 0)
         for q in range(4):
             nc.gpsimd.dma_start(out=wd_s[32 * q : 32 * q + 4, :], in_=wd_scales[0, 4 * q : 4 * q + 4, :].bitcast(I32))
+        nc.gpsimd.dma_start(out=wd_w[:], in_=wd_words[0].bitcast(I32))
 
         def cols(c, count=1):
             return slice(c * CHUNK, (c + count) * CHUNK)
@@ -81,15 +83,10 @@ def tile_list_modp_silu_none_kernel(
         def gather_scales(c, count=1):
             nc.vector.tensor_copy(v_s[:, cols(c, count)], tab_s[:].bitcast(U8).indirect(listed(c, count)))
 
-        def gather_words(c, count=1):
-            words = []
-            for a in range(PASSES):
-                v_w = ring.tile([P, count * CHUNK], U32, name="v_w%d" % a, align_bytes=64)
-                nc.vector.tensor_copy(v_w[:], tab_w[a][:].bitcast(U32).indirect(listed(c, count)))
-                words.append(v_w)
-            return words
+        def gather_words(a, c):
+            nc.vector.tensor_copy(v_w[a][:, cols(c)], tab_w[a][:].bitcast(U32).indirect(listed(c)))
 
-        def up(words, c, count=1):
+        def up(c, count=1):
             width = count * CHUNK
             act = ring.tile([P, PACK, width], F32, name="act")
             banks = [psum.tile([P, width], F32, name="up%d" % t) for t in range(PACK)]
@@ -99,7 +96,7 @@ def tile_list_modp_silu_none_kernel(
                         out=banks[t][:],
                         lhsT=wu_w[:, a, t * P : (t + 1) * P].bitcast(FP8X4),
                         lhsT_scale=wu_s[4 * a :, t * P : (t + 1) * P],
-                        rhs=words[a][:].bitcast(FP8X4),
+                        rhs=v_w[a][:, cols(c, count)].bitcast(FP8X4),
                         rhs_scale=v_s[4 * a :, cols(c, count)],
                         start=(a == 0),
                         stop=(a == PASSES - 1),
@@ -110,7 +107,7 @@ def tile_list_modp_silu_none_kernel(
 
         def smooth_on_vector(act):
             width = act.shape[2]
-            h = ring.tile([P, width, PACK], BF16, name="h", align_bytes=64)
+            h = keep.tile([P, width, PACK], BF16, name="h_early", align_bytes=64)
             nc.vector.tensor_tensor(
                 h[:], act[:].rearrange("p t j -> p j t"), sm_t[:].unsqueeze(1).to_broadcast([P, width, PACK]), MULT
             )
@@ -119,7 +116,7 @@ def tile_list_modp_silu_none_kernel(
         def smooth_on_scalar(act, tag):
             width = act.shape[2]
             planes = keep.tile([P, PACK, width], BF16, name="planes", tag=tag)
-            h = ring.tile([P, width, PACK], BF16, name="h", align_bytes=64)
+            h = keep.tile([P, width, PACK], BF16, name="h_late", align_bytes=64)
             for t in range(PACK):
                 nc.scalar.activation(out=planes[:, t, :], in_=act[:, t, :], func=ACT.Copy, scale=sm_t[:, t : t + 1])
             nc.scalar.copy(out=h[:], in_=planes[:].rearrange("p t j -> p j t"))
@@ -166,29 +163,28 @@ def tile_list_modp_silu_none_kernel(
 
         for c in range(CHUNKS):
             gather_scales(c)
-        words0 = gather_words(0)
-        words1 = gather_words(1)
+        for a in range(PASSES):
+            for c in range(CHUNKS):
+                gather_words(a, c)
 
-        for n in range(2):
-            for c0 in range(0, T, 1024):
-                nc.vector.memset(placed[n][:, c0 : c0 + 1024], 0.0)
-        for c0 in range(0, T, 512):
-            nc.gpsimd.memset(placed[2][:, c0 : c0 + 512], 0.0)
-        nc.gpsimd.dma_start(out=wd_w[:], in_=wd_words[0].bitcast(I32))
-        for c0 in range(0, T, 512):
-            nc.gpsimd.memset(placed[3][:, c0 : c0 + 512], 0.0)
+        for piece in range(2 * ROW_TILES):
+            half = placed[piece // 2][:, piece % 2 * 1024 : piece % 2 * 1024 + 1024]
+            if piece < 3:
+                nc.vector.memset(half, 0.0)
+            else:
+                nc.gpsimd.memset(half[:, :512], 0.0)
+                nc.gpsimd.memset(half[:, 512:], 0.0)
 
-        act = up(words0, 0)
-        words2 = gather_words(2, 2)
-        quantize(0, smooth_on_vector(act))
-        down(0, 0, 2, 0, 1, "y_a")
-        quantize(1, smooth_on_scalar(up(words1, 1), "stage1"))
-        down(1, 2, 2, 0, 1, "stage1")
-        act = up(words2, 2, 2)
-        down(2, 0, 2, 1, 1, "y_b")
-        down(3, 2, 1, 1, 1, "y_c")
+        quantize(0, smooth_on_vector(up(0)))
+        down(0, 0, 1, 0, 1, "y_a")
+        quantize(1, smooth_on_vector(up(1)))
+        down(1, 1, 1, 0, 1, "y_b")
+        down(2, 2, 2, 0, 1, "y_c")
+        act = up(2, 2)
+        down(3, 0, 2, 1, 1, "y_d")
+        down(0, 2, 1, 1, 1, "y_e")
         quantize(2, smooth_on_scalar(act, "stage2"), 2)
-        down(0, 3, 1, 1, 1, "stage2")
+        down(1, 3, 1, 1, 1, "stage2")
         for n in range(ROW_TILES):
-            down((n + 1) % 4, n, 1, 2, 2, "y%d" % n)
+            down((n + 2) % 4, n, 1, 2, 2, "y%d" % n)
             nc.sync.dma_start(out=out[n * P : (n + 1) * P, :], in_=placed[n][:])

@@ -37,16 +37,15 @@ def tile_list_modp_silu_none_kernel(
         offsets = keep.tile([P, J // LIST_ROWS], U16, name="offsets")
         tab_s = keep.tile([P, T // 4], I32, name="tab_s", align_bytes=64)
         wu_raw = keep.tile([P, PASSES, R], I32, name="wu_raw", tag="wu_then_wgo", align_bytes=64)
-        wu_s_raw = keep.tile([P, R // 4], I32, name="wu_s_raw", align_bytes=64)
+        wu_s_raw = keep.tile([P, R // 4], I32, name="wu_s_raw", tag="wu_s_then_wd", align_bytes=64)
         wu_w = keep.tile([P, PASSES, R], I32, name="wu_w", align_bytes=64)
         wu_s = keep.tile([P, R], U8, name="wu_s", align_bytes=64)
-        wd_w = keep.tile([P, N // 2], I32, name="wd_w", align_bytes=64)
         wd_s = keep.tile([P, N // 4], I32, name="wd_s", align_bytes=64)
         sm_t = keep.tile([P, PACK], F32, name="sm_t")
         v_s = keep.tile([P, J], U8, name="v_s", align_bytes=64)
         h_w = keep.tile([P, J], U32, name="h_w", align_bytes=64)
         h_s = keep.tile([P, J], U8, name="h_s", align_bytes=64)
-        placed = [keep.tile([P, T], F32, name="placed%d" % n) for n in range(ROW_TILES)]
+        placed = [keep.tile([P, T], F32, name="placed%d" % n) for n in range(2)]
         warm = keep.tile([P, 1], F32, name="warm", tag="tab_w0", align_bytes=64)
         warm_out = keep.tile([P, 1], F32, name="warm_out", tag="tab_w1", align_bytes=64)
         v_w = [keep.tile([P, J], U32, name="v_w%d" % a, align_bytes=64) for a in range(PASSES)]
@@ -68,11 +67,10 @@ def tile_list_modp_silu_none_kernel(
                 out=wu_s_raw[32 * q : 32 * q + 4 * PASSES, :], in_=wu_scales[:, 4 * q : 4 * q + 4, :].bitcast(I32)
             )
         nc.sync.dma_start(out=tab_w[1][:], in_=tab_words[1].rearrange("p t i -> p (t i)").bitcast(I32))
-        nc.gpsimd.dma_start(out=sm_t[:], in_=sm.rearrange("(p t) -> p t", t=PACK))
-        nc.gpsimd.memset(wd_s[:], 0)
+        nc.sync.dma_start(out=sm_t[:], in_=sm.rearrange("(p t) -> p t", t=PACK))
+        nc.vector.memset(wd_s[:], 0)
         for q in range(4):
-            nc.gpsimd.dma_start(out=wd_s[32 * q : 32 * q + 4, :], in_=wd_scales[0, 4 * q : 4 * q + 4, :].bitcast(I32))
-        nc.gpsimd.dma_start(out=wd_w[:], in_=wd_words[0].bitcast(I32))
+            nc.sync.dma_start(out=wd_s[32 * q : 32 * q + 4, :], in_=wd_scales[0, 4 * q : 4 * q + 4, :].bitcast(I32))
 
         def cols(c, count=1):
             return slice(c * CHUNK, (c + count) * CHUNK)
@@ -83,8 +81,8 @@ def tile_list_modp_silu_none_kernel(
         def gather_scales(c, count=1):
             nc.vector.tensor_copy(v_s[:, cols(c, count)], tab_s[:].bitcast(U8).indirect(listed(c, count)))
 
-        def gather_words(a, c):
-            nc.vector.tensor_copy(v_w[a][:, cols(c)], tab_w[a][:].bitcast(U32).indirect(listed(c)))
+        def gather_words(a, c, count=1):
+            nc.vector.tensor_copy(v_w[a][:, cols(c, count)], tab_w[a][:].bitcast(U32).indirect(listed(c, count)))
 
         def up(c, count=1):
             width = count * CHUNK
@@ -115,7 +113,7 @@ def tile_list_modp_silu_none_kernel(
 
         def smooth_on_scalar(act, tag):
             width = act.shape[2]
-            planes = keep.tile([P, PACK, width], BF16, name="planes", tag=tag)
+            planes = keep.tile([P, PACK, width], BF16, name="planes", tag=tag, align_bytes=64)
             h = keep.tile([P, width, PACK], BF16, name="h_late", align_bytes=64)
             for t in range(PACK):
                 nc.scalar.activation(out=planes[:, t, :], in_=act[:, t, :], func=ACT.Copy, scale=sm_t[:, t : t + 1])
@@ -141,7 +139,7 @@ def tile_list_modp_silu_none_kernel(
                     start=True,
                     stop=True,
                 )
-            y = keep.tile([P, tiles, count * CHUNK], F32, name="y", tag=tag)
+            y = keep.tile([P, tiles, count * CHUNK], F32, name="y", tag=tag, align_bytes=64)
             nc.scalar.copy(out=y[:], in_=bank[:])
             for n in range(n0, n0 + tiles):
                 place(n, y[:, n - n0, :], c, count)
@@ -157,28 +155,33 @@ def tile_list_modp_silu_none_kernel(
         wgo_t = keep.tile([P, J], F32, name="wgo_t", tag="wu_then_wgo", align_bytes=64)
         nc.sync.dma_start(out=wgo_t[:], in_=wgo)
         nc.vector.tensor_copy(
-            out=wu_s[:].rearrange("p (t m) -> p m t", t=PACK),
-            in_=wu_s_raw[:].bitcast(U8).rearrange("p (m t) -> p m t", t=PACK),
+            out=wu_s[:].rearrange("p (t m) -> p t m", t=PACK),
+            in_=wu_s_raw[:].bitcast(U8).rearrange("p (m t) -> p t m", t=PACK),
         )
+        wd_w = keep.tile([P, N // 2], I32, name="wd_w", tag="wu_s_then_wd", align_bytes=64)
+        nc.sync.dma_start(out=wd_w[:], in_=wd_words[0].bitcast(I32))
 
-        for c in range(CHUNKS):
-            gather_scales(c)
-        for a in range(PASSES):
-            for c in range(CHUNKS):
-                gather_words(a, c)
+        gather_scales(0, CHUNKS)
+        gather_words(0, 0, CHUNKS)
+        gather_words(1, 0)
+        gather_words(1, 1)
+        gather_words(1, 2, 2)
 
-        for piece in range(2 * ROW_TILES):
-            half = placed[piece // 2][:, piece % 2 * 1024 : piece % 2 * 1024 + 1024]
-            if piece < 3:
-                nc.vector.memset(half, 0.0)
-            else:
-                nc.gpsimd.memset(half[:, :512], 0.0)
-                nc.gpsimd.memset(half[:, 512:], 0.0)
+        for n in range(2):
+            for c0 in range(0, T, 1024):
+                nc.vector.memset(placed[n][:, c0 : c0 + 1024], 0.0)
+
+        def zeroed_on_gpsimd(tag):
+            tile = keep.tile([P, T], F32, name="placed_late", tag=tag, align_bytes=64)
+            nc.gpsimd.memset(tile[:], 0.0)
+            return tile
 
         quantize(0, smooth_on_vector(up(0)))
         down(0, 0, 1, 0, 1, "y_a")
         quantize(1, smooth_on_vector(up(1)))
         down(1, 1, 1, 0, 1, "y_b")
+        placed.append(zeroed_on_gpsimd("h_early"))
+        placed.append(zeroed_on_gpsimd("y_a"))
         down(2, 2, 2, 0, 1, "y_c")
         act = up(2, 2)
         down(3, 0, 2, 1, 1, "y_d")

@@ -23,6 +23,7 @@ CHUNK = 256
 CHUNKS = J // CHUNK
 ROW_TILES = N // P
 LIST_ROWS = 16
+BANK = 512
 
 
 def tile_list_modp_silu_none_kernel(
@@ -31,46 +32,42 @@ def tile_list_modp_silu_none_kernel(
     nc = tc.nc
     with ExitStack() as ctx:
         keep = ctx.enter_context(tc.tile_pool(name="keep", bufs=1))
-        ring = ctx.enter_context(tc.tile_pool(name="ring", bufs=2))
+        shared = ctx.enter_context(tc.tile_pool(name="shared", bufs=1))
         psum = ctx.enter_context(tc.psum_pool(name="psum", bufs=1))
 
+        def sbuf(name, shape, dtype, tag=None):
+            return keep.tile(shape, dtype, name=name, tag=tag or name, align_bytes=64)
+
         offsets = keep.tile([P, J // LIST_ROWS], U16, name="offsets")
-        tab_s = keep.tile([P, T // 4], I32, name="tab_s", align_bytes=64)
-        wu_raw = keep.tile([P, PASSES, R], I32, name="wu_raw", tag="wu_then_wgo", align_bytes=64)
-        wu_s_raw = keep.tile([P, R // 4], I32, name="wu_s_raw", tag="wu_s_then_wd", align_bytes=64)
-        wu_w = keep.tile([P, PASSES, R], I32, name="wu_w", align_bytes=64)
-        wu_s = keep.tile([P, R], U8, name="wu_s", align_bytes=64)
-        wd_s = keep.tile([P, N // 4], I32, name="wd_s", align_bytes=64)
-        sm_t = keep.tile([P, PACK], F32, name="sm_t")
-        v_s = keep.tile([P, J], U8, name="v_s", align_bytes=64)
-        h_w = keep.tile([P, J], U32, name="h_w", align_bytes=64)
-        h_s = keep.tile([P, J], U8, name="h_s", align_bytes=64)
-        placed = [keep.tile([P, T], F32, name="placed%d" % n) for n in range(2)]
-        warm = keep.tile([P, 1], F32, name="warm", tag="tab_w0", align_bytes=64)
-        warm_out = keep.tile([P, 1], F32, name="warm_out", tag="tab_w1", align_bytes=64)
-        v_w = [keep.tile([P, J], U32, name="v_w%d" % a, align_bytes=64) for a in range(PASSES)]
+        tab_s = sbuf("tab_s", [P, T // 4], I32)
+        wu_raw = sbuf("wu_raw", [P, PASSES, R], I32)
+        wu_w = sbuf("wu_w", [P, PASSES, R], I32)
+        wu_s = sbuf("wu_s", [P, R], U8)
+        sm_t = sbuf("sm_t", [P, PACK], F32)
+        v_s = sbuf("v_s", [P, J], U8)
+        h_first = sbuf("h_first", [P, CHUNK], U32)
+        h_rest = sbuf("h_rest", [P, J - CHUNK], U32)
+        h_s = sbuf("h_s", [P, J], U8)
+        windows = [sbuf("window%d" % n, [P, T], F32) for n in range(2)]
+        warm = sbuf("warm", [P, 1], F32, "tab_w0")
+        warm_out = sbuf("warm_out", [P, 1], F32, "tab_w1")
 
         nc.gpsimd.memset(tab_s[:], 0)
         nc.vector.memset(warm[:], 0.0)
-        nc.vector.memset(wu_s_raw[:], 0)
         nc.scalar.activation(out=warm_out[:], in_=warm[:], func=ACT.Silu)
-        tab_w = [keep.tile([P, T], I32, name="tab_w%d" % a, align_bytes=64) for a in range(PASSES)]
+        for window in windows:
+            nc.vector.memset(window[:], 0.0)
+
+        tab_w = [sbuf("tab_w%d" % a, [P, T], I32) for a in range(PASSES)]
         nc.sync.dma_start(offsets[:], offs)
         nc.sync.dma_start(out=wu_raw[:], in_=wu_words.rearrange("a p r i -> p a (r i)").bitcast(I32))
+        nc.sync.dma_start(out=sm_t[:], in_=sm.rearrange("(p t) -> p t", t=PACK))
         for q in range(4):
             nc.sync.dma_start(
                 out=tab_s[32 * q : 32 * q + 4 * PASSES, :], in_=tab_scales[:, 4 * q : 4 * q + 4, :].bitcast(I32)
             )
-        nc.sync.dma_start(out=tab_w[0][:], in_=tab_words[0].rearrange("p t i -> p (t i)").bitcast(I32))
-        for q in range(4):
-            nc.sync.dma_start(
-                out=wu_s_raw[32 * q : 32 * q + 4 * PASSES, :], in_=wu_scales[:, 4 * q : 4 * q + 4, :].bitcast(I32)
-            )
-        nc.sync.dma_start(out=tab_w[1][:], in_=tab_words[1].rearrange("p t i -> p (t i)").bitcast(I32))
-        nc.sync.dma_start(out=sm_t[:], in_=sm.rearrange("(p t) -> p t", t=PACK))
-        nc.vector.memset(wd_s[:], 0)
-        for q in range(4):
-            nc.sync.dma_start(out=wd_s[32 * q : 32 * q + 4, :], in_=wd_scales[0, 4 * q : 4 * q + 4, :].bitcast(I32))
+        for a in range(PASSES):
+            nc.sync.dma_start(out=tab_w[a][:], in_=tab_words[a].rearrange("p t i -> p (t i)").bitcast(I32))
 
         def cols(c, count=1):
             return slice(c * CHUNK, (c + count) * CHUNK)
@@ -78,116 +75,147 @@ def tile_list_modp_silu_none_kernel(
         def listed(c, count=1):
             return offsets[:, c * CHUNK // LIST_ROWS : (c + count) * CHUNK // LIST_ROWS]
 
-        def gather_scales(c, count=1):
-            nc.vector.tensor_copy(v_s[:, cols(c, count)], tab_s[:].bitcast(U8).indirect(listed(c, count)))
+        v_w = {}
 
-        def gather_words(a, c, count=1):
-            nc.vector.tensor_copy(v_w[a][:, cols(c, count)], tab_w[a][:].bitcast(U32).indirect(listed(c, count)))
+        def gather_words(a, c, count=1, tile=None):
+            if tile is None:
+                tile = sbuf("v_w%d_%d" % (a, c), [P, count * CHUNK], U32)
+            nc.vector.tensor_copy(tile[:], tab_w[a][:].bitcast(U32).indirect(listed(c, count)))
+            for i in range(count):
+                v_w[a, c + i] = tile[:, i * CHUNK : (i + 1) * CHUNK]
 
-        def up(c, count=1):
-            width = count * CHUNK
-            act = ring.tile([P, PACK, width], F32, name="act")
-            banks = [psum.tile([P, width], F32, name="up%d" % t) for t in range(PACK)]
-            for a in range(PASSES):
-                for t in range(PACK):
-                    nc.tensor.matmul_mx(
-                        out=banks[t][:],
-                        lhsT=wu_w[:, a, t * P : (t + 1) * P].bitcast(FP8X4),
-                        lhsT_scale=wu_s[4 * a :, t * P : (t + 1) * P],
-                        rhs=v_w[a][:, cols(c, count)].bitcast(FP8X4),
-                        rhs_scale=v_s[4 * a :, cols(c, count)],
-                        start=(a == 0),
-                        stop=(a == PASSES - 1),
-                    )
-            for t in range(PACK):
-                nc.scalar.activation(out=act[:, t, :], in_=banks[t][:], func=ACT.Silu)
-            return act
+        def up_pass(a, bank, slices, c, j0, width, opening):
+            for i, t in enumerate(slices):
+                nc.tensor.matmul_mx(
+                    out=bank[:, i, :],
+                    lhsT=wu_w[:, a, t * P : (t + 1) * P].bitcast(FP8X4),
+                    lhsT_scale=wu_s[4 * a :, t * P : (t + 1) * P],
+                    rhs=v_w[a, c][:, j0 : j0 + width].bitcast(FP8X4),
+                    rhs_scale=v_s[4 * a :, c * CHUNK + j0 : c * CHUNK + j0 + width],
+                    start=(opening and i == 0),
+                    stop=(not opening and i == len(slices) - 1),
+                )
 
-        def smooth_on_vector(act):
-            width = act.shape[2]
-            h = keep.tile([P, width, PACK], BF16, name="h_early", align_bytes=64)
-            nc.vector.tensor_tensor(
-                h[:], act[:].rearrange("p t j -> p j t"), sm_t[:].unsqueeze(1).to_broadcast([P, width, PACK]), MULT
-            )
-            return h
+        def up_banks(shape, numbers):
+            return [psum.tile(shape, F32, name="up", tag="bank%d" % b) for b in numbers]
 
-        def smooth_on_scalar(act, tag):
-            width = act.shape[2]
-            planes = keep.tile([P, PACK, width], BF16, name="planes", tag=tag, align_bytes=64)
-            h = keep.tile([P, width, PACK], BF16, name="h_late", align_bytes=64)
+        def up_by_slices(c, numbers):
+            banks = up_banks([P, 2, CHUNK], numbers)
+            for b in range(2):
+                for a in (1, 0):
+                    up_pass(a, banks[b], (2 * b, 2 * b + 1), c, 0, CHUNK, a == 1)
+            return banks
+
+        def smooth_on_scalar(c, banks, planes_tag):
+            act = sbuf("act%d" % c, [P, PACK, CHUNK], F32, "act")
+            planes = sbuf("planes%d" % c, [P, PACK, CHUNK], BF16, planes_tag)
+            h = sbuf("h%d" % c, [P, CHUNK, PACK], BF16)
+            for b in range(2):
+                nc.scalar.activation(out=act[:, 2 * b : 2 * b + 2, :], in_=banks[b][:], func=ACT.Silu)
             for t in range(PACK):
                 nc.scalar.activation(out=planes[:, t, :], in_=act[:, t, :], func=ACT.Copy, scale=sm_t[:, t : t + 1])
             nc.scalar.copy(out=h[:], in_=planes[:].rearrange("p t j -> p j t"))
             return h
 
-        def quantize(c, h, count=1):
+        def h_words(c, count=1):
+            return h_first[:] if c == 0 else h_rest[:, cols(c - 1, count)]
+
+        def quantize(c, h):
             nc.vector.quantize_mx(
-                out=h_w[:, cols(c, count)].bitcast(FP8X4),
-                scales=h_s[:, cols(c, count)],
-                in_=h[:].rearrange("p j t -> p (j t)"),
+                out=h_words(c).bitcast(FP8X4), scales=h_s[:, cols(c)], in_=h[:].rearrange("p j t -> p (j t)")
             )
 
-        def down(slot, n0, tiles, c, count, tag):
-            bank = psum.tile([P, tiles, count * CHUNK], F32, name="down%d" % slot)
-            for n in range(n0, n0 + tiles):
-                nc.tensor.matmul_mx(
-                    out=bank[:, n - n0, :],
-                    lhsT=wd_w[:, n * P // 2 : (n + 1) * P // 2].bitcast(U8).bitcast(FP4X4),
-                    lhsT_scale=wd_s[:].bitcast(U8)[:, n * P : (n + 1) * P],
-                    rhs=h_w[:, cols(c, count)].bitcast(FP8X4),
-                    rhs_scale=h_s[:, cols(c, count)],
-                    start=True,
-                    stop=True,
-                )
-            y = keep.tile([P, tiles, count * CHUNK], F32, name="y", tag=tag, align_bytes=64)
+        def down(n, c, number, count=1):
+            bank = psum.tile([P, count * CHUNK], F32, name="down", tag="bank%d" % number)
+            nc.tensor.matmul_mx(
+                out=bank[:],
+                lhsT=wd_w[:, n * P // 2 : (n + 1) * P // 2].bitcast(U8).bitcast(FP4X4),
+                lhsT_scale=wd_s.bitcast(U8)[:, n * P : (n + 1) * P],
+                rhs=h_words(c, count).bitcast(FP8X4),
+                rhs_scale=h_s[:, cols(c, count)],
+                start=True,
+                stop=True,
+            )
+            return bank
+
+        def place(window, y, c, count):
+            nc.vector.tensor_tensor(window[:].indirect(listed(c, count)), y, wgo_t[:, cols(c, count)], MULT)
+
+        def copy_and_place(n, c, bank, count=1, tag=None):
+            y = sbuf("y%d_%d" % (n, c), [P, count * CHUNK], F32, tag)
             nc.scalar.copy(out=y[:], in_=bank[:])
-            for n in range(n0, n0 + tiles):
-                place(n, y[:, n - n0, :], c, count)
+            place(windows[n], y[:], c, count)
 
-        def place(n, y, c, count):
-            nc.vector.tensor_tensor(
-                placed[n][:].indirect(listed(c, count)), y, wgo_t[:, cols(c, count)], MULT
-            )
+        def store(n, window):
+            nc.sync.dma_start(out=out[n * P : (n + 1) * P, :], in_=window[:])
 
         nc.vector.tensor_copy(
             out=wu_w[:].rearrange("p a (t m) -> p a m t", t=PACK), in_=wu_raw[:].rearrange("p a (m t) -> p a m t", t=PACK)
         )
-        wgo_t = keep.tile([P, J], F32, name="wgo_t", tag="wu_then_wgo", align_bytes=64)
-        nc.sync.dma_start(out=wgo_t[:], in_=wgo)
+        wu_s_raw = sbuf("wu_s_raw", [P, R // 4], I32, "wu_raw")
+        nc.vector.memset(wu_s_raw[:], 0)
+        for q in range(4):
+            nc.scalar.dma_start(
+                out=wu_s_raw[32 * q : 32 * q + 4 * PASSES, :], in_=wu_scales[:, 4 * q : 4 * q + 4, :].bitcast(I32)
+            )
+        nc.vector.tensor_copy(v_s[:], tab_s[:].bitcast(U8).indirect(offsets[:]))
+        wd = sbuf("wd", [P, N // 2 + N // 4], I32, "tab_s")
+        wd_w = wd[:, : N // 2]
+        wd_s = wd[:, N // 2 :]
+        nc.vector.memset(wd_s, 0)
+        nc.scalar.dma_start(out=wd_w, in_=wd_words[0].bitcast(I32))
+        for q in range(4):
+            nc.scalar.dma_start(out=wd_s[32 * q : 32 * q + 4, :], in_=wd_scales[0, 4 * q : 4 * q + 4, :].bitcast(I32))
         nc.vector.tensor_copy(
             out=wu_s[:].rearrange("p (t m) -> p t m", t=PACK),
             in_=wu_s_raw[:].bitcast(U8).rearrange("p (m t) -> p t m", t=PACK),
         )
-        wd_w = keep.tile([P, N // 2], I32, name="wd_w", tag="wu_s_then_wd", align_bytes=64)
-        nc.sync.dma_start(out=wd_w[:], in_=wd_words[0].bitcast(I32))
-
-        gather_scales(0, CHUNKS)
-        gather_words(0, 0, CHUNKS)
+        gather_words(0, 0)
+        gather_words(0, 1, CHUNKS - 1, sbuf("v_w0_1", [P, J - CHUNK], U32, "wu_raw"))
+        wgo_t = sbuf("wgo_t", [P, J], F32, "tab_w0")
+        nc.sync.dma_start(out=wgo_t[:], in_=wgo)
         gather_words(1, 0)
         gather_words(1, 1)
-        gather_words(1, 2, 2)
+        gather_words(1, 3)
 
+        half = CHUNK // 2
+        first = up_banks([P, PACK, half], (0, 1))
+        for b in range(2):
+            up_pass(0, first[b], range(PACK), 0, b * half, half, True)
+        h0 = shared.tile([P, CHUNK, PACK], BF16, name="h0", offset=0, align_bytes=64)
+        for b in range(2):
+            up_pass(1, first[b], range(PACK), 0, b * half, half, False)
+            act = sbuf("act0_%d" % b, [P, half, PACK], F32)
+            nc.scalar.activation(out=act[:], in_=first[b][:].rearrange("p t j -> p j t"), func=ACT.Silu)
+            nc.vector.tensor_tensor(
+                h0[:, b * half : (b + 1) * half, :], act[:], sm_t[:].unsqueeze(1).to_broadcast([P, half, PACK]), MULT
+            )
+        quantize(0, h0)
+        gather_words(1, 2, 1, shared.tile([P, CHUNK], U32, name="v_w1_2", offset=0, align_bytes=64))
+        second = up_by_slices(1, (2, 3))
+        sums = [down(n, 0, 4 + n) for n in range(ROW_TILES)]
+        copy_and_place(0, 0, sums[0])
+        copy_and_place(1, 0, sums[1])
+        windows.append(shared.tile([P, T], F32, name="window2", offset=4 * CHUNK, align_bytes=64))
+        for c0 in range(0, T, T // 2):
+            nc.vector.memset(windows[2][:, c0 : c0 + T // 2], 0.0)
+        quantize(1, smooth_on_scalar(1, second, "h_first"))
+        copy_and_place(2, 0, sums[2], 1, "h_first")
+        copy_and_place(0, 1, down(0, 1, 2))
+        copy_and_place(1, 1, down(1, 1, 3))
+        quantize(2, smooth_on_scalar(2, up_by_slices(2, (0, 1)), "planes2"))
+        copy_and_place(2, 1, down(2, 1, 4), 1, "planes2")
+        copy_and_place(0, 2, down(0, 2, 0))
+        quantize(3, smooth_on_scalar(3, up_by_slices(3, (2, 3)), "planes3"))
+        copy_and_place(1, 2, down(1, 2, 1), 1, "planes3")
         for n in range(2):
-            for c0 in range(0, T, 1024):
-                nc.vector.memset(placed[n][:, c0 : c0 + 1024], 0.0)
-
-        def zeroed_on_gpsimd(tag):
-            tile = keep.tile([P, T], F32, name="placed_late", tag=tag, align_bytes=64)
-            nc.gpsimd.memset(tile[:], 0.0)
-            return tile
-
-        quantize(0, smooth_on_vector(up(0)))
-        down(0, 0, 1, 0, 1, "y_a")
-        quantize(1, smooth_on_vector(up(1)))
-        down(1, 1, 1, 0, 1, "y_b")
-        placed.append(zeroed_on_gpsimd("h_early"))
-        placed.append(zeroed_on_gpsimd("y_a"))
-        down(2, 2, 2, 0, 1, "y_c")
-        act = up(2, 2)
-        down(3, 0, 2, 1, 1, "y_d")
-        down(0, 2, 1, 1, 1, "y_e")
-        quantize(2, smooth_on_scalar(act, "stage2"), 2)
-        down(1, 3, 1, 1, 1, "stage2")
-        for n in range(ROW_TILES):
-            down((n + 2) % 4, n, 1, 2, 2, "y%d" % n)
-            nc.sync.dma_start(out=out[n * P : (n + 1) * P, :], in_=placed[n][:])
+            copy_and_place(n, 3, down(n, 3, 5 + n))
+            store(n, windows[n])
+        copy_and_place(2, 2, down(2, 2, 4, 2), 2)
+        store(2, windows[2])
+        y_last = sbuf("y_last", [P, J], F32)
+        nc.scalar.copy(out=y_last[:, cols(0)], in_=sums[3][:])
+        nc.scalar.copy(out=y_last[:, cols(1)], in_=down(3, 1, 2)[:])
+        nc.scalar.copy(out=y_last[:, cols(2, 2)], in_=down(3, 2, 3, 2)[:])
+        place(windows[0], y_last[:], 0, CHUNKS)
+        store(3, windows[0])

@@ -33,6 +33,7 @@ def tile_list_modp_silu_none_kernel(
     with ExitStack() as ctx:
         keep = ctx.enter_context(tc.tile_pool(name="keep", bufs=1))
         shared = ctx.enter_context(tc.tile_pool(name="shared", bufs=1))
+        reused = ctx.enter_context(tc.tile_pool(name="reused", bufs=1))
         psum = ctx.enter_context(tc.psum_pool(name="psum", bufs=1))
 
         def sbuf(name, shape, dtype, tag=None):
@@ -41,6 +42,7 @@ def tile_list_modp_silu_none_kernel(
         offsets = keep.tile([P, J // LIST_ROWS], U16, name="offsets")
         tab_s = sbuf("tab_s", [P, T // 4], I32)
         wu_raw = sbuf("wu_raw", [P, PASSES, R], I32)
+        wu_s_raw = sbuf("wu_s_raw", [P, R // 4], I32)
         wu_w = sbuf("wu_w", [P, PASSES, R], I32)
         wu_s = sbuf("wu_s", [P, R], U8)
         sm_t = sbuf("sm_t", [P, PACK], F32)
@@ -49,22 +51,27 @@ def tile_list_modp_silu_none_kernel(
         h_rest = sbuf("h_rest", [P, J - CHUNK], U32)
         h_s = sbuf("h_s", [P, J], U8)
         windows = [sbuf("window%d" % n, [P, T], F32) for n in range(2)]
-        warm = sbuf("warm", [P, 1], F32, "tab_w0")
+        warm = reused.tile([P, 1], F32, name="warm", offset=0, align_bytes=64)
         warm_out = sbuf("warm_out", [P, 1], F32, "tab_w1")
 
         nc.gpsimd.memset(tab_s[:], 0)
         nc.vector.memset(warm[:], 0.0)
+        nc.vector.memset(wu_s_raw[:], 0)
         nc.scalar.activation(out=warm_out[:], in_=warm[:], func=ACT.Silu)
         for window in windows:
             nc.vector.memset(window[:], 0.0)
 
-        tab_w = [sbuf("tab_w%d" % a, [P, T], I32) for a in range(PASSES)]
+        tab_w = [reused.tile([P, T], I32, name="tab_w0", offset=0, align_bytes=64), sbuf("tab_w1", [P, T], I32)]
         nc.sync.dma_start(offsets[:], offs)
         nc.sync.dma_start(out=wu_raw[:], in_=wu_words.rearrange("a p r i -> p a (r i)").bitcast(I32))
         nc.sync.dma_start(out=sm_t[:], in_=sm.rearrange("(p t) -> p t", t=PACK))
         for q in range(4):
             nc.sync.dma_start(
                 out=tab_s[32 * q : 32 * q + 4 * PASSES, :], in_=tab_scales[:, 4 * q : 4 * q + 4, :].bitcast(I32)
+            )
+        for q in range(4):
+            nc.sync.dma_start(
+                out=wu_s_raw[32 * q : 32 * q + 4 * PASSES, :], in_=wu_scales[:, 4 * q : 4 * q + 4, :].bitcast(I32)
             )
         for a in range(PASSES):
             nc.sync.dma_start(out=tab_w[a][:], in_=tab_words[a].rearrange("p t i -> p (t i)").bitcast(I32))
@@ -130,7 +137,7 @@ def tile_list_modp_silu_none_kernel(
             nc.tensor.matmul_mx(
                 out=bank[:],
                 lhsT=wd_w[:, n * P // 2 : (n + 1) * P // 2].bitcast(U8).bitcast(FP4X4),
-                lhsT_scale=wd_s.bitcast(U8)[:, n * P : (n + 1) * P],
+                lhsT_scale=wd_s[:].bitcast(U8)[:, n * P : (n + 1) * P],
                 rhs=h_words(c, count).bitcast(FP8X4),
                 rhs_scale=h_s[:, cols(c, count)],
                 start=True,
@@ -152,27 +159,20 @@ def tile_list_modp_silu_none_kernel(
         nc.vector.tensor_copy(
             out=wu_w[:].rearrange("p a (t m) -> p a m t", t=PACK), in_=wu_raw[:].rearrange("p a (m t) -> p a m t", t=PACK)
         )
-        wu_s_raw = sbuf("wu_s_raw", [P, R // 4], I32, "wu_raw")
-        nc.vector.memset(wu_s_raw[:], 0)
-        for q in range(4):
-            nc.scalar.dma_start(
-                out=wu_s_raw[32 * q : 32 * q + 4 * PASSES, :], in_=wu_scales[:, 4 * q : 4 * q + 4, :].bitcast(I32)
-            )
         nc.vector.tensor_copy(v_s[:], tab_s[:].bitcast(U8).indirect(offsets[:]))
-        wd = sbuf("wd", [P, N // 2 + N // 4], I32, "tab_s")
-        wd_w = wd[:, : N // 2]
-        wd_s = wd[:, N // 2 :]
-        nc.vector.memset(wd_s, 0)
-        nc.scalar.dma_start(out=wd_w, in_=wd_words[0].bitcast(I32))
-        for q in range(4):
-            nc.scalar.dma_start(out=wd_s[32 * q : 32 * q + 4, :], in_=wd_scales[0, 4 * q : 4 * q + 4, :].bitcast(I32))
         nc.vector.tensor_copy(
             out=wu_s[:].rearrange("p (t m) -> p t m", t=PACK),
             in_=wu_s_raw[:].bitcast(U8).rearrange("p (m t) -> p t m", t=PACK),
         )
         gather_words(0, 0)
-        gather_words(0, 1, CHUNKS - 1, sbuf("v_w0_1", [P, J - CHUNK], U32, "wu_raw"))
-        wgo_t = sbuf("wgo_t", [P, J], F32, "tab_w0")
+        gather_words(0, 1, CHUNKS - 1)
+        wd_s = reused.tile([P, N // 4], I32, name="wd_s", offset=0, align_bytes=64)
+        wd_w = reused.tile([P, N // 2], I32, name="wd_w", offset=N, align_bytes=64)
+        wgo_t = reused.tile([P, J], F32, name="wgo_t", offset=4 * J, align_bytes=64)
+        nc.gpsimd.memset(wd_s[:], 0)
+        nc.sync.dma_start(out=wd_w[:], in_=wd_words[0].bitcast(I32))
+        for q in range(4):
+            nc.sync.dma_start(out=wd_s[32 * q : 32 * q + 4, :], in_=wd_scales[0, 4 * q : 4 * q + 4, :].bitcast(I32))
         nc.sync.dma_start(out=wgo_t[:], in_=wgo)
         gather_words(1, 0)
         gather_words(1, 1)

@@ -42,26 +42,29 @@ def tile_list_modp_silu_none_kernel(
         offsets = keep.tile([P, J // LIST_ROWS], U16, name="offsets")
         tab_s = sbuf("tab_s", [P, T // 4], I32)
         wu_raw = sbuf("wu_raw", [P, PASSES, R], I32)
-        wu_s_raw = sbuf("wu_s_raw", [P, R // 4], I32)
         wu_w = sbuf("wu_w", [P, PASSES, R], I32)
         wu_s = sbuf("wu_s", [P, R], U8)
         sm_t = sbuf("sm_t", [P, PACK], F32)
-        v_s = sbuf("v_s", [P, J], U8)
         h_first = sbuf("h_first", [P, CHUNK], U32)
         h_rest = sbuf("h_rest", [P, J - CHUNK], U32)
         h_s = sbuf("h_s", [P, J], U8)
         windows = [sbuf("window%d" % n, [P, T], F32) for n in range(2)]
-        warm = reused.tile([P, 1], F32, name="warm", offset=0, align_bytes=64)
+        zeros = reused.tile([P, R // 4], I32, name="zeros", offset=0, align_bytes=64)
+        wu_s_raw = sbuf("wu_s_raw", [P, R // 4], I32)
+        warm = sbuf("warm", [P, 1], F32)
         warm_out = sbuf("warm_out", [P, 1], F32, "tab_w1")
 
-        nc.gpsimd.memset(tab_s[:], 0)
         nc.vector.memset(warm[:], 0.0)
-        nc.vector.memset(wu_s_raw[:], 0)
+        nc.vector.memset(zeros[:], 0)
+        nc.vector.memset(tab_s[:], 0)
+        nc.vector.tensor_copy(wu_s_raw[:], zeros[:])
         nc.scalar.activation(out=warm_out[:], in_=warm[:], func=ACT.Silu)
-        for window in windows:
-            nc.vector.memset(window[:], 0.0)
 
         tab_w = [reused.tile([P, T], I32, name="tab_w0", offset=0, align_bytes=64), sbuf("tab_w1", [P, T], I32)]
+
+        def load_table(a):
+            nc.sync.dma_start(out=tab_w[a][:], in_=tab_words[a].rearrange("p t i -> p (t i)").bitcast(I32))
+
         nc.sync.dma_start(offsets[:], offs)
         nc.sync.dma_start(out=wu_raw[:], in_=wu_words.rearrange("a p r i -> p a (r i)").bitcast(I32))
         nc.sync.dma_start(out=sm_t[:], in_=sm.rearrange("(p t) -> p t", t=PACK))
@@ -69,12 +72,16 @@ def tile_list_modp_silu_none_kernel(
             nc.sync.dma_start(
                 out=tab_s[32 * q : 32 * q + 4 * PASSES, :], in_=tab_scales[:, 4 * q : 4 * q + 4, :].bitcast(I32)
             )
+        load_table(0)
         for q in range(4):
             nc.sync.dma_start(
                 out=wu_s_raw[32 * q : 32 * q + 4 * PASSES, :], in_=wu_scales[:, 4 * q : 4 * q + 4, :].bitcast(I32)
             )
-        for a in range(PASSES):
-            nc.sync.dma_start(out=tab_w[a][:], in_=tab_words[a].rearrange("p t i -> p (t i)").bitcast(I32))
+        load_table(1)
+        wd_s = sbuf("wd_s", [P, N // 4], I32, "warm")
+        nc.vector.memset(wd_s[:], 0)
+        for q in range(4):
+            nc.sync.dma_start(out=wd_s[32 * q : 32 * q + 4, :], in_=wd_scales[0, 4 * q : 4 * q + 4, :].bitcast(I32))
 
         def cols(c, count=1):
             return slice(c * CHUNK, (c + count) * CHUNK)
@@ -106,11 +113,14 @@ def tile_list_modp_silu_none_kernel(
         def up_banks(shape, numbers):
             return [psum.tile(shape, F32, name="up", tag="bank%d" % b) for b in numbers]
 
-        def up_by_slices(c, numbers):
-            banks = up_banks([P, 2, CHUNK], numbers)
+        def up_by_slices(a, c, banks, opening):
             for b in range(2):
-                for a in (1, 0):
-                    up_pass(a, banks[b], (2 * b, 2 * b + 1), c, 0, CHUNK, a == 1)
+                up_pass(a, banks[b], (2 * b, 2 * b + 1), c, 0, CHUNK, opening)
+
+        def up_late(c, numbers):
+            banks = up_banks([P, 2, CHUNK], numbers)
+            up_by_slices(1, c, banks, True)
+            up_by_slices(0, c, banks, False)
             return banks
 
         def smooth_on_scalar(c, banks, planes_tag):
@@ -157,22 +167,25 @@ def tile_list_modp_silu_none_kernel(
             nc.sync.dma_start(out=out[n * P : (n + 1) * P, :], in_=window[:])
 
         nc.vector.tensor_copy(
-            out=wu_w[:].rearrange("p a (t m) -> p a m t", t=PACK), in_=wu_raw[:].rearrange("p a (m t) -> p a m t", t=PACK)
+            out=wu_w[:].rearrange("p a (t m i) -> p a m t i", t=PACK, i=4),
+            in_=wu_raw[:].rearrange("p a (m i t) -> p a m t i", t=PACK, i=4),
         )
+        v_s = sbuf("v_s", [P, J], U8)
+        for window in windows:
+            for c0 in range(0, T, T // 2):
+                nc.vector.memset(window[:, c0 : c0 + T // 2], 0.0)
         nc.vector.tensor_copy(v_s[:], tab_s[:].bitcast(U8).indirect(offsets[:]))
         nc.vector.tensor_copy(
             out=wu_s[:].rearrange("p (t m) -> p t m", t=PACK),
             in_=wu_s_raw[:].bitcast(U8).rearrange("p (m t) -> p t m", t=PACK),
         )
         gather_words(0, 0)
-        gather_words(0, 1, CHUNKS - 1)
-        wd_s = reused.tile([P, N // 4], I32, name="wd_s", offset=0, align_bytes=64)
-        wd_w = reused.tile([P, N // 2], I32, name="wd_w", offset=N, align_bytes=64)
+        later = sbuf("v_w0_later", [P, J - CHUNK], U32, "wu_s_raw")
+        gather_words(0, 1, 1, later[:, :CHUNK])
+        gather_words(0, 2, 2, later[:, CHUNK:])
+        wd_w = reused.tile([P, N // 2], I32, name="wd_w", offset=0, align_bytes=64)
         wgo_t = reused.tile([P, J], F32, name="wgo_t", offset=4 * J, align_bytes=64)
-        nc.gpsimd.memset(wd_s[:], 0)
         nc.sync.dma_start(out=wd_w[:], in_=wd_words[0].bitcast(I32))
-        for q in range(4):
-            nc.sync.dma_start(out=wd_s[32 * q : 32 * q + 4, :], in_=wd_scales[0, 4 * q : 4 * q + 4, :].bitcast(I32))
         nc.sync.dma_start(out=wgo_t[:], in_=wgo)
         gather_words(1, 0)
         gather_words(1, 1)
@@ -182,6 +195,8 @@ def tile_list_modp_silu_none_kernel(
         first = up_banks([P, PACK, half], (0, 1))
         for b in range(2):
             up_pass(0, first[b], range(PACK), 0, b * half, half, True)
+        second = up_banks([P, 2, CHUNK], (2, 3))
+        up_by_slices(0, 1, second, True)
         h0 = shared.tile([P, CHUNK, PACK], BF16, name="h0", offset=0, align_bytes=64)
         for b in range(2):
             up_pass(1, first[b], range(PACK), 0, b * half, half, False)
@@ -192,21 +207,20 @@ def tile_list_modp_silu_none_kernel(
             )
         quantize(0, h0)
         gather_words(1, 2, 1, shared.tile([P, CHUNK], U32, name="v_w1_2", offset=0, align_bytes=64))
-        second = up_by_slices(1, (2, 3))
+        up_by_slices(1, 1, second, False)
         sums = [down(n, 0, 4 + n) for n in range(ROW_TILES)]
         copy_and_place(0, 0, sums[0])
         copy_and_place(1, 0, sums[1])
         windows.append(shared.tile([P, T], F32, name="window2", offset=4 * CHUNK, align_bytes=64))
-        for c0 in range(0, T, T // 2):
-            nc.vector.memset(windows[2][:, c0 : c0 + T // 2], 0.0)
+        nc.gpsimd.memset(windows[2][:], 0.0)
         quantize(1, smooth_on_scalar(1, second, "h_first"))
         copy_and_place(2, 0, sums[2], 1, "h_first")
         copy_and_place(0, 1, down(0, 1, 2))
         copy_and_place(1, 1, down(1, 1, 3))
-        quantize(2, smooth_on_scalar(2, up_by_slices(2, (0, 1)), "planes2"))
+        quantize(2, smooth_on_scalar(2, up_late(2, (0, 1)), "planes2"))
         copy_and_place(2, 1, down(2, 1, 4), 1, "planes2")
         copy_and_place(0, 2, down(0, 2, 0))
-        quantize(3, smooth_on_scalar(3, up_by_slices(3, (2, 3)), "planes3"))
+        quantize(3, smooth_on_scalar(3, up_late(3, (2, 3)), "planes3"))
         copy_and_place(1, 2, down(1, 2, 1), 1, "planes3")
         for n in range(2):
             copy_and_place(n, 3, down(n, 3, 5 + n))

@@ -34,6 +34,7 @@ def tile_list_modp_silu_none_kernel(
         keep = ctx.enter_context(tc.tile_pool(name="keep", bufs=1))
         shared = ctx.enter_context(tc.tile_pool(name="shared", bufs=1))
         reused = ctx.enter_context(tc.tile_pool(name="reused", bufs=1))
+        after_scales = ctx.enter_context(tc.tile_pool(name="after_scales", bufs=1))
         psum = ctx.enter_context(tc.psum_pool(name="psum", bufs=1))
 
         def sbuf(name, shape, dtype, tag=None):
@@ -48,9 +49,10 @@ def tile_list_modp_silu_none_kernel(
         h_first = sbuf("h_first", [P, CHUNK], U32)
         h_rest = sbuf("h_rest", [P, J - CHUNK], U32)
         h_s = sbuf("h_s", [P, J], U8)
-        windows = [sbuf("window%d" % n, [P, T], F32) for n in range(2)]
+        windows = [sbuf("window0", [P, T], F32)]
         zeros = reused.tile([P, R // 4], I32, name="zeros", offset=0, align_bytes=64)
-        wu_s_raw = sbuf("wu_s_raw", [P, R // 4], I32)
+        spanning = after_scales.tile([P, N // 2 + 32], I32, name="wu_s_raw", offset=4 * CHUNK - 64, align_bytes=64)
+        wu_s_raw = spanning[:, : R // 4]
         warm = sbuf("warm", [P, 1], F32)
         warm_out = sbuf("warm_out", [P, 1], F32, "tab_w1")
 
@@ -117,10 +119,10 @@ def tile_list_modp_silu_none_kernel(
             for b in range(2):
                 up_pass(a, banks[b], (2 * b, 2 * b + 1), c, 0, CHUNK, opening)
 
-        def up_late(c, numbers):
+        def up_late(c, numbers, order):
             banks = up_banks([P, 2, CHUNK], numbers)
-            up_by_slices(1, c, banks, True)
-            up_by_slices(0, c, banks, False)
+            up_by_slices(order[0], c, banks, True)
+            up_by_slices(order[1], c, banks, False)
             return banks
 
         def smooth_on_scalar(c, banks, planes_tag):
@@ -171,33 +173,28 @@ def tile_list_modp_silu_none_kernel(
             in_=wu_raw[:].rearrange("p a (m i t) -> p a m t i", t=PACK, i=4),
         )
         v_s = sbuf("v_s", [P, J], U8)
-        for window in windows:
-            for c0 in range(0, T, T // 2):
-                nc.vector.memset(window[:, c0 : c0 + T // 2], 0.0)
+        for c0 in range(0, T, T // 2):
+            nc.vector.memset(windows[0][:, c0 : c0 + T // 2], 0.0)
         nc.vector.tensor_copy(v_s[:], tab_s[:].bitcast(U8).indirect(offsets[:]))
         nc.vector.tensor_copy(
             out=wu_s[:].rearrange("p (t m) -> p t m", t=PACK),
             in_=wu_s_raw[:].bitcast(U8).rearrange("p (m t) -> p t m", t=PACK),
         )
         gather_words(0, 0)
-        later = sbuf("v_w0_later", [P, J - CHUNK], U32, "wu_s_raw")
-        gather_words(0, 1, 1, later[:, :CHUNK])
-        gather_words(0, 2, 2, later[:, CHUNK:])
-        wd_w = reused.tile([P, N // 2], I32, name="wd_w", offset=0, align_bytes=64)
-        wgo_t = reused.tile([P, J], F32, name="wgo_t", offset=4 * J, align_bytes=64)
+        gather_words(0, 1, 1, after_scales.tile([P, CHUNK], U32, name="v_w0_1", offset=0, align_bytes=64))
+        wd_w = after_scales.tile([P, N // 2], I32, name="wd_w", offset=4 * CHUNK, align_bytes=64)
+        wgo_t = after_scales.tile([P, J], F32, name="wgo_t", offset=4 * CHUNK + 2 * N, align_bytes=64)
         nc.sync.dma_start(out=wd_w[:], in_=wd_words[0].bitcast(I32))
         nc.sync.dma_start(out=wgo_t[:], in_=wgo)
         gather_words(1, 0)
         gather_words(1, 1)
-        gather_words(1, 3)
+        gather_words(1, 2, 2)
 
         half = CHUNK // 2
         first = up_banks([P, PACK, half], (0, 1))
         for b in range(2):
             up_pass(0, first[b], range(PACK), 0, b * half, half, True)
-        second = up_banks([P, 2, CHUNK], (2, 3))
-        up_by_slices(0, 1, second, True)
-        h0 = shared.tile([P, CHUNK, PACK], BF16, name="h0", offset=0, align_bytes=64)
+        h0 = shared.tile([P, CHUNK + 16, PACK], BF16, name="h0", offset=4 * T - 64, align_bytes=64)
         for b in range(2):
             up_pass(1, first[b], range(PACK), 0, b * half, half, False)
             act = sbuf("act0_%d" % b, [P, half, PACK], F32)
@@ -205,22 +202,23 @@ def tile_list_modp_silu_none_kernel(
             nc.vector.tensor_tensor(
                 h0[:, b * half : (b + 1) * half, :], act[:], sm_t[:].unsqueeze(1).to_broadcast([P, half, PACK]), MULT
             )
-        quantize(0, h0)
-        gather_words(1, 2, 1, shared.tile([P, CHUNK], U32, name="v_w1_2", offset=0, align_bytes=64))
-        up_by_slices(1, 1, second, False)
+        quantize(0, h0[:, :CHUNK, :])
+        gather_words(0, 2, 2, shared.tile([P, 2 * CHUNK], U32, name="v_w0_2", offset=4 * T, align_bytes=64))
+        for n, offset in ((1, 0), (2, 4 * T + 8 * CHUNK)):
+            windows.append(shared.tile([P, T], F32, name="window%d" % n, offset=offset, align_bytes=64))
+            nc.gpsimd.memset(windows[n][:], 0.0)
+        second = up_late(1, (2, 3), (1, 0))
         sums = [down(n, 0, 4 + n) for n in range(ROW_TILES)]
         copy_and_place(0, 0, sums[0])
         copy_and_place(1, 0, sums[1])
-        windows.append(shared.tile([P, T], F32, name="window2", offset=4 * CHUNK, align_bytes=64))
-        nc.gpsimd.memset(windows[2][:], 0.0)
         quantize(1, smooth_on_scalar(1, second, "h_first"))
         copy_and_place(2, 0, sums[2], 1, "h_first")
         copy_and_place(0, 1, down(0, 1, 2))
         copy_and_place(1, 1, down(1, 1, 3))
-        quantize(2, smooth_on_scalar(2, up_late(2, (0, 1)), "planes2"))
+        quantize(2, smooth_on_scalar(2, up_late(2, (0, 1), (0, 1)), "planes2"))
         copy_and_place(2, 1, down(2, 1, 4), 1, "planes2")
         copy_and_place(0, 2, down(0, 2, 0))
-        quantize(3, smooth_on_scalar(3, up_late(3, (2, 3)), "planes3"))
+        quantize(3, smooth_on_scalar(3, up_late(3, (2, 3), (0, 1)), "planes3"))
         copy_and_place(1, 2, down(1, 2, 1), 1, "planes3")
         for n in range(2):
             copy_and_place(n, 3, down(n, 3, 5 + n))

@@ -32,7 +32,6 @@ def tile_list_modp_silu_none_kernel(
     nc = tc.nc
     with ExitStack() as ctx:
         keep = ctx.enter_context(tc.tile_pool(name="keep", bufs=1))
-        shared = ctx.enter_context(tc.tile_pool(name="shared", bufs=1))
         reused = ctx.enter_context(tc.tile_pool(name="reused", bufs=1))
         after_scales = ctx.enter_context(tc.tile_pool(name="after_scales", bufs=1))
         psum = ctx.enter_context(tc.psum_pool(name="psum", bufs=1))
@@ -49,7 +48,7 @@ def tile_list_modp_silu_none_kernel(
         h_first = sbuf("h_first", [P, CHUNK], U32)
         h_rest = sbuf("h_rest", [P, J - CHUNK], U32)
         h_s = sbuf("h_s", [P, J], U8)
-        windows = [sbuf("window0", [P, T], F32)]
+        windows = [sbuf("window%d" % n, [P, T], F32) for n in range(3)]
         zeros = reused.tile([P, R // 4], I32, name="zeros", offset=0, align_bytes=64)
         spanning = after_scales.tile([P, N // 2 + 32], I32, name="wu_s_raw", offset=4 * CHUNK - 64, align_bytes=64)
         wu_s_raw = spanning[:, : R // 4]
@@ -168,13 +167,14 @@ def tile_list_modp_silu_none_kernel(
         def store(n, window):
             nc.sync.dma_start(out=out[n * P : (n + 1) * P, :], in_=window[:])
 
+        for window in windows:
+            for c0 in range(0, T, T // 2):
+                nc.vector.memset(window[:, c0 : c0 + T // 2], 0.0)
         nc.vector.tensor_copy(
             out=wu_w[:].rearrange("p a (t m i) -> p a m t i", t=PACK, i=4),
             in_=wu_raw[:].rearrange("p a (m i t) -> p a m t i", t=PACK, i=4),
         )
         v_s = sbuf("v_s", [P, J], U8)
-        for c0 in range(0, T, T // 2):
-            nc.vector.memset(windows[0][:, c0 : c0 + T // 2], 0.0)
         nc.vector.tensor_copy(v_s[:], tab_s[:].bitcast(U8).indirect(offsets[:]))
         nc.vector.tensor_copy(
             out=wu_s[:].rearrange("p (t m) -> p t m", t=PACK),
@@ -194,7 +194,7 @@ def tile_list_modp_silu_none_kernel(
         first = up_banks([P, PACK, half], (0, 1))
         for b in range(2):
             up_pass(0, first[b], range(PACK), 0, b * half, half, True)
-        h0 = shared.tile([P, CHUNK + 16, PACK], BF16, name="h0", offset=4 * T - 64, align_bytes=64)
+        h0 = sbuf("h0", [P, CHUNK, PACK], BF16)
         for b in range(2):
             up_pass(1, first[b], range(PACK), 0, b * half, half, False)
             act = sbuf("act0_%d" % b, [P, half, PACK], F32)
@@ -202,11 +202,8 @@ def tile_list_modp_silu_none_kernel(
             nc.vector.tensor_tensor(
                 h0[:, b * half : (b + 1) * half, :], act[:], sm_t[:].unsqueeze(1).to_broadcast([P, half, PACK]), MULT
             )
-        quantize(0, h0[:, :CHUNK, :])
-        gather_words(0, 2, 2, shared.tile([P, 2 * CHUNK], U32, name="v_w0_2", offset=4 * T, align_bytes=64))
-        for n, offset in ((1, 0), (2, 4 * T + 8 * CHUNK)):
-            windows.append(shared.tile([P, T], F32, name="window%d" % n, offset=offset, align_bytes=64))
-            nc.gpsimd.memset(windows[n][:], 0.0)
+        quantize(0, h0)
+        gather_words(0, 2, 2, sbuf("v_w0_2", [P, 2 * CHUNK], U32, "h0"))
         second = up_late(1, (2, 3), (1, 0))
         sums = [down(n, 0, 4 + n) for n in range(ROW_TILES)]
         copy_and_place(0, 0, sums[0])

@@ -20,10 +20,14 @@ P = 128
 PACK = 4
 PASSES = K // (P * PACK)
 CHUNK = 256
+HALF = CHUNK // 2
 CHUNKS = J // CHUNK
 ROW_TILES = N // P
+WINDOWS = ROW_TILES - 1
 LIST_ROWS = 16
-BANK = 512
+QUADRANTS = 4
+LINE = 4
+ALIGN = 64
 
 
 def tile_list_modp_silu_none_kernel(
@@ -37,7 +41,7 @@ def tile_list_modp_silu_none_kernel(
         psum = ctx.enter_context(tc.psum_pool(name="psum", bufs=1))
 
         def sbuf(name, shape, dtype, tag=None):
-            return keep.tile(shape, dtype, name=name, tag=tag or name, align_bytes=64)
+            return keep.tile(shape, dtype, name=name, tag=tag or name, align_bytes=ALIGN)
 
         offsets = keep.tile([P, J // LIST_ROWS], U16, name="offsets")
         tab_s = sbuf("tab_s", [P, T // 4], I32)
@@ -48,9 +52,13 @@ def tile_list_modp_silu_none_kernel(
         h_first = sbuf("h_first", [P, CHUNK], U32)
         h_rest = sbuf("h_rest", [P, J - CHUNK], U32)
         h_s = sbuf("h_s", [P, J], U8)
-        windows = [sbuf("window%d" % n, [P, T], F32) for n in range(3)]
-        zeros = reused.tile([P, R // 4], I32, name="zeros", offset=0, align_bytes=64)
-        spanning = after_scales.tile([P, N // 2 + 32], I32, name="wu_s_raw", offset=4 * CHUNK - 64, align_bytes=64)
+        windows = [sbuf("window%d" % n, [P, T], F32) for n in range(WINDOWS)]
+        zeros = reused.tile([P, R // 4], I32, name="zeros", offset=0, align_bytes=ALIGN)
+        wd_at = 4 * CHUNK
+        wgo_at = wd_at + 2 * N
+        spanning = after_scales.tile(
+            [P, (2 * N + 2 * ALIGN) // 4], I32, name="wu_s_raw", offset=wd_at - ALIGN, align_bytes=ALIGN
+        )
         wu_s_raw = spanning[:, : R // 4]
         warm = sbuf("warm", [P, 1], F32)
         warm_out = sbuf("warm_out", [P, 1], F32, "tab_w1")
@@ -61,28 +69,24 @@ def tile_list_modp_silu_none_kernel(
         nc.vector.tensor_copy(wu_s_raw[:], zeros[:])
         nc.scalar.activation(out=warm_out[:], in_=warm[:], func=ACT.Silu)
 
-        tab_w = [reused.tile([P, T], I32, name="tab_w0", offset=0, align_bytes=64), sbuf("tab_w1", [P, T], I32)]
+        tab_w = [reused.tile([P, T], I32, name="tab_w0", offset=0, align_bytes=ALIGN), sbuf("tab_w1", [P, T], I32)]
 
         def load_table(a):
             nc.sync.dma_start(out=tab_w[a][:], in_=tab_words[a].rearrange("p t i -> p (t i)").bitcast(I32))
 
+        def load_scales(tile, scales):
+            for q in range(QUADRANTS):
+                nc.sync.dma_start(
+                    out=tile[32 * q : 32 * q + 4 * PASSES, :], in_=scales[:, 4 * q : 4 * q + 4, :].bitcast(I32)
+                )
+
         nc.sync.dma_start(offsets[:], offs)
         nc.sync.dma_start(out=wu_raw[:], in_=wu_words.rearrange("a p r i -> p a (r i)").bitcast(I32))
         nc.sync.dma_start(out=sm_t[:], in_=sm.rearrange("(p t) -> p t", t=PACK))
-        for q in range(4):
-            nc.sync.dma_start(
-                out=tab_s[32 * q : 32 * q + 4 * PASSES, :], in_=tab_scales[:, 4 * q : 4 * q + 4, :].bitcast(I32)
-            )
+        load_scales(tab_s, tab_scales)
         load_table(0)
-        for q in range(4):
-            nc.sync.dma_start(
-                out=wu_s_raw[32 * q : 32 * q + 4 * PASSES, :], in_=wu_scales[:, 4 * q : 4 * q + 4, :].bitcast(I32)
-            )
+        load_scales(wu_s_raw, wu_scales)
         load_table(1)
-        wd_s = sbuf("wd_s", [P, N // 4], I32, "warm")
-        nc.vector.memset(wd_s[:], 0)
-        for q in range(4):
-            nc.sync.dma_start(out=wd_s[32 * q : 32 * q + 4, :], in_=wd_scales[0, 4 * q : 4 * q + 4, :].bitcast(I32))
 
         def cols(c, count=1):
             return slice(c * CHUNK, (c + count) * CHUNK)
@@ -114,25 +118,25 @@ def tile_list_modp_silu_none_kernel(
         def up_banks(shape, numbers):
             return [psum.tile(shape, F32, name="up", tag="bank%d" % b) for b in numbers]
 
-        def up_by_slices(a, c, banks, opening):
-            for b in range(2):
-                up_pass(a, banks[b], (2 * b, 2 * b + 1), c, 0, CHUNK, opening)
-
-        def up_late(c, numbers, order):
+        def up(c, numbers, opening_pass):
             banks = up_banks([P, 2, CHUNK], numbers)
-            up_by_slices(order[0], c, banks, True)
-            up_by_slices(order[1], c, banks, False)
+            for a in (opening_pass, 1 - opening_pass):
+                for b in range(2):
+                    up_pass(a, banks[b], (2 * b, 2 * b + 1), c, 0, CHUNK, a == opening_pass)
             return banks
 
-        def smooth_on_scalar(c, banks, planes_tag):
+        def smooth_on_scalar(c, banks, slices_tag):
             act = sbuf("act%d" % c, [P, PACK, CHUNK], F32, "act")
-            planes = sbuf("planes%d" % c, [P, PACK, CHUNK], BF16, planes_tag)
+            by_slice = sbuf("planes%d" % c, [P, PACK, CHUNK], BF16, slices_tag)
             h = sbuf("h%d" % c, [P, CHUNK, PACK], BF16)
             for b in range(2):
                 nc.scalar.activation(out=act[:, 2 * b : 2 * b + 2, :], in_=banks[b][:], func=ACT.Silu)
             for t in range(PACK):
-                nc.scalar.activation(out=planes[:, t, :], in_=act[:, t, :], func=ACT.Copy, scale=sm_t[:, t : t + 1])
-            nc.scalar.copy(out=h[:], in_=planes[:].rearrange("p t j -> p j t"))
+                nc.scalar.activation(out=by_slice[:, t, :], in_=act[:, t, :], func=ACT.Copy, scale=sm_t[:, t : t + 1])
+            nc.scalar.copy(
+                out=h[:].rearrange("p (c i) t -> p c t i", i=LINE),
+                in_=by_slice[:].rearrange("p t (c i) -> p c t i", i=LINE),
+            )
             return h
 
         def h_words(c, count=1):
@@ -170,9 +174,13 @@ def tile_list_modp_silu_none_kernel(
         for window in windows:
             for c0 in range(0, T, T // 2):
                 nc.vector.memset(window[:, c0 : c0 + T // 2], 0.0)
+        wd_s = sbuf("wd_s", [P, N // 4], I32)
+        nc.vector.memset(wd_s[:], 0)
+        for q in range(QUADRANTS):
+            nc.sync.dma_start(out=wd_s[32 * q : 32 * q + 4, :], in_=wd_scales[0, 4 * q : 4 * q + 4, :].bitcast(I32))
         nc.vector.tensor_copy(
-            out=wu_w[:].rearrange("p a (t m i) -> p a m t i", t=PACK, i=4),
-            in_=wu_raw[:].rearrange("p a (m i t) -> p a m t i", t=PACK, i=4),
+            out=wu_w[:].rearrange("p a (t m i) -> p a m t i", t=PACK, i=LINE),
+            in_=wu_raw[:].rearrange("p a (m i t) -> p a m t i", t=PACK, i=LINE),
         )
         v_s = sbuf("v_s", [P, J], U8)
         nc.vector.tensor_copy(v_s[:], tab_s[:].bitcast(U8).indirect(offsets[:]))
@@ -181,30 +189,30 @@ def tile_list_modp_silu_none_kernel(
             in_=wu_s_raw[:].bitcast(U8).rearrange("p (m t) -> p t m", t=PACK),
         )
         gather_words(0, 0)
-        gather_words(0, 1, 1, after_scales.tile([P, CHUNK], U32, name="v_w0_1", offset=0, align_bytes=64))
-        wd_w = after_scales.tile([P, N // 2], I32, name="wd_w", offset=4 * CHUNK, align_bytes=64)
-        wgo_t = after_scales.tile([P, J], F32, name="wgo_t", offset=4 * CHUNK + 2 * N, align_bytes=64)
+        gather_words(0, 1, 1, after_scales.tile([P, CHUNK], U32, name="v_w0_1", offset=0, align_bytes=ALIGN))
+        wd_w = after_scales.tile([P, N // 2], I32, name="wd_w", offset=wd_at, align_bytes=ALIGN)
+        wgo_t = after_scales.tile([P, J], F32, name="wgo_t", offset=wgo_at, align_bytes=ALIGN)
         nc.sync.dma_start(out=wd_w[:], in_=wd_words[0].bitcast(I32))
         nc.sync.dma_start(out=wgo_t[:], in_=wgo)
         gather_words(1, 0)
         gather_words(1, 1)
         gather_words(1, 2, 2)
 
-        half = CHUNK // 2
-        first = up_banks([P, PACK, half], (0, 1))
+        first = up_banks([P, PACK, HALF], (0, 1))
         for b in range(2):
-            up_pass(0, first[b], range(PACK), 0, b * half, half, True)
+            up_pass(0, first[b], range(PACK), 0, b * HALF, HALF, True)
         h0 = sbuf("h0", [P, CHUNK, PACK], BF16)
         for b in range(2):
-            up_pass(1, first[b], range(PACK), 0, b * half, half, False)
-            act = sbuf("act0_%d" % b, [P, half, PACK], F32)
+            up_pass(1, first[b], range(PACK), 0, b * HALF, HALF, False)
+            act = sbuf("act0_%d" % b, [P, HALF, PACK], F32)
             nc.scalar.activation(out=act[:], in_=first[b][:].rearrange("p t j -> p j t"), func=ACT.Silu)
             nc.vector.tensor_tensor(
-                h0[:, b * half : (b + 1) * half, :], act[:], sm_t[:].unsqueeze(1).to_broadcast([P, half, PACK]), MULT
+                h0[:, b * HALF : (b + 1) * HALF, :], act[:], sm_t[:].unsqueeze(1).to_broadcast([P, HALF, PACK]), MULT
             )
         quantize(0, h0)
         gather_words(0, 2, 2, sbuf("v_w0_2", [P, 2 * CHUNK], U32, "h0"))
-        second = up_late(1, (2, 3), (1, 0))
+
+        second = up(1, (2, 3), 1)
         sums = [down(n, 0, 4 + n) for n in range(ROW_TILES)]
         copy_and_place(0, 0, sums[0])
         copy_and_place(1, 0, sums[1])
@@ -212,11 +220,12 @@ def tile_list_modp_silu_none_kernel(
         copy_and_place(2, 0, sums[2], 1, "h_first")
         copy_and_place(0, 1, down(0, 1, 2))
         copy_and_place(1, 1, down(1, 1, 3))
-        quantize(2, smooth_on_scalar(2, up_late(2, (0, 1), (0, 1)), "planes2"))
+        quantize(2, smooth_on_scalar(2, up(2, (0, 1), 0), "planes2"))
         copy_and_place(2, 1, down(2, 1, 4), 1, "planes2")
         copy_and_place(0, 2, down(0, 2, 0))
-        quantize(3, smooth_on_scalar(3, up_late(3, (2, 3), (0, 1)), "planes3"))
+        quantize(3, smooth_on_scalar(3, up(3, (2, 3), 0), "planes3"))
         copy_and_place(1, 2, down(1, 2, 1), 1, "planes3")
+
         for n in range(2):
             copy_and_place(n, 3, down(n, 3, 5 + n))
             store(n, windows[n])

@@ -23,7 +23,7 @@ CHUNK = 256
 HALF = CHUNK // 2
 CHUNKS = J // CHUNK
 ROW_TILES = N // P
-WINDOWS = ROW_TILES - 1
+WINDOWS = ROW_TILES
 LIST_ROWS = 16
 QUADRANTS = 4
 LINE = 4
@@ -45,19 +45,19 @@ def tile_list_modp_silu_none_kernel(
 
         offsets = keep.tile([P, J // LIST_ROWS], U16, name="offsets")
         tab_s = sbuf("tab_s", [P, T // 4], I32)
-        wu_raw = sbuf("wu_raw", [P, PASSES, R], I32)
+        wu_raw = reused.tile([P, PASSES, R], I32, name="wu_raw", offset=4 * T, align_bytes=ALIGN)
         wu_w = sbuf("wu_w", [P, PASSES, R], I32)
         wu_s = sbuf("wu_s", [P, R], U8)
         sm_t = sbuf("sm_t", [P, PACK], F32)
         h_first = sbuf("h_first", [P, CHUNK], U32)
         h_rest = sbuf("h_rest", [P, J - CHUNK], U32)
         h_s = sbuf("h_s", [P, J], U8)
-        windows = [sbuf("window%d" % n, [P, T], F32) for n in range(WINDOWS)]
+        windows = [sbuf("window%d" % n, [P, T], F32) for n in range(2)]
         zeros = reused.tile([P, R // 4], I32, name="zeros", offset=0, align_bytes=ALIGN)
         wd_at = 4 * CHUNK
         wgo_at = wd_at + 2 * N
         spanning = after_scales.tile(
-            [P, (2 * N + 2 * ALIGN) // 4], I32, name="wu_s_raw", offset=wd_at - ALIGN, align_bytes=ALIGN
+            [P, (2 * N + 4 * J + 2 * ALIGN) // 4], I32, name="wu_s_raw", offset=wd_at - ALIGN, align_bytes=ALIGN
         )
         wu_s_raw = spanning[:, : R // 4]
         warm = sbuf("warm", [P, 1], F32)
@@ -125,14 +125,20 @@ def tile_list_modp_silu_none_kernel(
                     up_pass(a, banks[b], (2 * b, 2 * b + 1), c, 0, CHUNK, a == opening_pass)
             return banks
 
-        def smooth_on_scalar(c, banks, slices_tag):
+        def silu(c, banks):
             act = sbuf("act%d" % c, [P, PACK, CHUNK], F32, "act")
-            by_slice = sbuf("planes%d" % c, [P, PACK, CHUNK], BF16, slices_tag)
-            h = sbuf("h%d" % c, [P, CHUNK, PACK], BF16)
             for b in range(2):
                 nc.scalar.activation(out=act[:, 2 * b : 2 * b + 2, :], in_=banks[b][:], func=ACT.Silu)
+            return act
+
+        def scale(c, act, slices_tag):
+            by_slice = sbuf("planes%d" % c, [P, PACK, CHUNK], BF16, slices_tag)
             for t in range(PACK):
                 nc.scalar.activation(out=by_slice[:, t, :], in_=act[:, t, :], func=ACT.Copy, scale=sm_t[:, t : t + 1])
+            return by_slice
+
+        def weave(c, by_slice):
+            h = sbuf("h%d" % c, [P, CHUNK, PACK], BF16)
             nc.scalar.copy(
                 out=h[:].rearrange("p (c i) t -> p c t i", i=LINE),
                 in_=by_slice[:].rearrange("p t (c i) -> p c t i", i=LINE),
@@ -182,12 +188,18 @@ def tile_list_modp_silu_none_kernel(
             out=wu_w[:].rearrange("p a (t m i) -> p a m t i", t=PACK, i=LINE),
             in_=wu_raw[:].rearrange("p a (m i t) -> p a m t i", t=PACK, i=LINE),
         )
+        windows.append(reused.tile([P, T], F32, name="window2", offset=4 * T, align_bytes=ALIGN))
+        for c0 in range(0, T, T // 4):
+            nc.gpsimd.memset(windows[2][:, c0 : c0 + T // 4], 0.0)
         v_s = sbuf("v_s", [P, J], U8)
         nc.vector.tensor_copy(v_s[:], tab_s[:].bitcast(U8).indirect(offsets[:]))
         nc.vector.tensor_copy(
             out=wu_s[:].rearrange("p (t m) -> p t m", t=PACK),
             in_=wu_s_raw[:].bitcast(U8).rearrange("p (m t) -> p t m", t=PACK),
         )
+        windows.append(after_scales.tile([P, T], F32, name="window3", offset=wgo_at + 4 * J, align_bytes=ALIGN))
+        for c0 in range(0, T, T // 4):
+            nc.gpsimd.memset(windows[3][:, c0 : c0 + T // 4], 0.0)
         gather_words(0, 0)
         gather_words(0, 1, 1, after_scales.tile([P, CHUNK], U32, name="v_w0_1", offset=0, align_bytes=ALIGN))
         wd_w = after_scales.tile([P, N // 2], I32, name="wd_w", offset=wd_at, align_bytes=ALIGN)
@@ -212,28 +224,24 @@ def tile_list_modp_silu_none_kernel(
         quantize(0, h0)
         gather_words(0, 2, 2, sbuf("v_w0_2", [P, 2 * CHUNK], U32, "h0"))
 
-        second = up(1, (2, 3), 1)
+        act = silu(1, up(1, (2, 3), 1))
         sums = [down(n, 0, 4 + n) for n in range(ROW_TILES)]
-        copy_and_place(0, 0, sums[0])
-        copy_and_place(1, 0, sums[1])
-        quantize(1, smooth_on_scalar(1, second, "h_first"))
-        copy_and_place(2, 0, sums[2], 1, "h_first")
-        copy_and_place(0, 1, down(0, 1, 2))
-        copy_and_place(1, 1, down(1, 1, 3))
-        quantize(2, smooth_on_scalar(2, up(2, (0, 1), 0), "planes2"))
-        copy_and_place(2, 1, down(2, 1, 4), 1, "planes2")
-        copy_and_place(0, 2, down(0, 2, 0))
-        quantize(3, smooth_on_scalar(3, up(3, (2, 3), 0), "planes3"))
-        copy_and_place(1, 2, down(1, 2, 1), 1, "planes3")
-
+        for n in range(3):
+            copy_and_place(n, 0, sums[n])
+        quantize(1, weave(1, scale(1, act, "h_first")))
+        copy_and_place(3, 0, sums[3], 1, "h_first")
+        act = silu(2, up(2, (0, 1), 0))
+        for n in range(3):
+            copy_and_place(n, 1, down(n, 1, 4 + n))
+        quantize(2, weave(2, scale(2, act, "planes2")))
+        copy_and_place(3, 1, down(3, 1, 7), 1, "planes2")
+        by_slice = scale(3, silu(3, up(3, (2, 3), 0)), "planes3")
+        copy_and_place(0, 2, down(0, 2, 4))
+        quantize(3, weave(3, by_slice))
+        copy_and_place(1, 2, down(1, 2, 5), 1, "planes3")
         for n in range(2):
-            copy_and_place(n, 3, down(n, 3, 5 + n))
+            copy_and_place(n, 3, down(n, 3, n))
             store(n, windows[n])
-        copy_and_place(2, 2, down(2, 2, 4, 2), 2)
-        store(2, windows[2])
-        y_last = sbuf("y_last", [P, J], F32)
-        nc.scalar.copy(out=y_last[:, cols(0)], in_=sums[3][:])
-        nc.scalar.copy(out=y_last[:, cols(1)], in_=down(3, 1, 2)[:])
-        nc.scalar.copy(out=y_last[:, cols(2, 2)], in_=down(3, 2, 3, 2)[:])
-        place(windows[0], y_last[:], 0, CHUNKS)
-        store(3, windows[0])
+        for n in range(2, 4):
+            copy_and_place(n, 2, down(n, 2, 4 + n, 2), 2)
+            store(n, windows[n])

@@ -38,6 +38,7 @@ def tile_list_modp_silu_none_kernel(
         keep = ctx.enter_context(tc.tile_pool(name="keep", bufs=1))
         reused = ctx.enter_context(tc.tile_pool(name="reused", bufs=1))
         after_scales = ctx.enter_context(tc.tile_pool(name="after_scales", bufs=1))
+        after_words = ctx.enter_context(tc.tile_pool(name="after_words", bufs=1))
         psum = ctx.enter_context(tc.psum_pool(name="psum", bufs=1))
 
         def sbuf(name, shape, dtype, tag=None):
@@ -45,27 +46,32 @@ def tile_list_modp_silu_none_kernel(
 
         offsets = keep.tile([P, J // LIST_ROWS], U16, name="offsets")
         tab_s = sbuf("tab_s", [P, T // 4], I32)
-        wu_raw = reused.tile([P, PASSES, R], I32, name="wu_raw", offset=4 * T, align_bytes=ALIGN)
+        sm_at = 4 * T
+        wd_s_at = sm_at + ALIGN
+        window3_at = wd_s_at + N
+        raw0_at = sm_at - 4 * R
+        wu_raw0 = after_words.tile(
+            [P, (window3_at + ALIGN - raw0_at) // 4], I32, name="wu_raw0", offset=raw0_at, align_bytes=ALIGN
+        )[:, :R]
         wu_w = sbuf("wu_w", [P, PASSES, R], I32)
         wu_s = sbuf("wu_s", [P, R], U8)
-        sm_t = sbuf("sm_t", [P, PACK], F32)
         h_first = sbuf("h_first", [P, CHUNK], U32)
         h_rest = sbuf("h_rest", [P, J - CHUNK], U32)
         h_s = sbuf("h_s", [P, J], U8)
         windows = [sbuf("window%d" % n, [P, T], F32) for n in range(2)]
         zeros = reused.tile([P, R // 4], I32, name="zeros", offset=0, align_bytes=ALIGN)
-        wd_at = 4 * CHUNK
+        wd_at = 8 * CHUNK
         wgo_at = wd_at + 2 * N
         spanning = after_scales.tile(
-            [P, (2 * N + 4 * J + 2 * ALIGN) // 4], I32, name="wu_s_raw", offset=wd_at - ALIGN, align_bytes=ALIGN
+            [P, (2 * N + 2 * ALIGN) // 4], I32, name="wu_s_raw", offset=wd_at - ALIGN, align_bytes=ALIGN
         )
         wu_s_raw = spanning[:, : R // 4]
         warm = sbuf("warm", [P, 1], F32)
         warm_out = sbuf("warm_out", [P, 1], F32, "tab_w1")
 
-        nc.vector.memset(warm[:], 0.0)
-        nc.vector.memset(zeros[:], 0)
         nc.vector.memset(tab_s[:], 0)
+        nc.vector.memset(zeros[:], 0)
+        nc.vector.memset(warm[:], 0.0)
         nc.vector.tensor_copy(wu_s_raw[:], zeros[:])
         nc.scalar.activation(out=warm_out[:], in_=warm[:], func=ACT.Silu)
 
@@ -81,11 +87,12 @@ def tile_list_modp_silu_none_kernel(
                 )
 
         nc.sync.dma_start(offsets[:], offs)
-        nc.sync.dma_start(out=wu_raw[:], in_=wu_words.rearrange("a p r i -> p a (r i)").bitcast(I32))
-        nc.sync.dma_start(out=sm_t[:], in_=sm.rearrange("(p t) -> p t", t=PACK))
+        nc.sync.dma_start(out=wu_raw0, in_=wu_words[0].rearrange("p r i -> p (r i)").bitcast(I32))
         load_scales(tab_s, tab_scales)
-        load_table(0)
         load_scales(wu_s_raw, wu_scales)
+        load_table(0)
+        wu_raw1 = sbuf("wu_raw1", [P, R], I32, "warm")
+        nc.sync.dma_start(out=wu_raw1[:], in_=wu_words[1].rearrange("p r i -> p (r i)").bitcast(I32))
         load_table(1)
 
         def cols(c, count=1):
@@ -153,14 +160,15 @@ def tile_list_modp_silu_none_kernel(
                 out=h_words(c).bitcast(FP8X4), scales=h_s[:, cols(c)], in_=h[:].rearrange("p j t -> p (j t)")
             )
 
-        def down(n, c, number, count=1):
-            bank = psum.tile([P, count * CHUNK], F32, name="down", tag="bank%d" % number)
+        def down(n, c, number, count=1, j0=0, width=None):
+            width = width or count * CHUNK
+            bank = psum.tile([P, width], F32, name="down", tag="bank%d" % number)
             nc.tensor.matmul_mx(
                 out=bank[:],
                 lhsT=wd_w[:, n * P // 2 : (n + 1) * P // 2].bitcast(U8).bitcast(FP4X4),
                 lhsT_scale=wd_s[:].bitcast(U8)[:, n * P : (n + 1) * P],
-                rhs=h_words(c, count).bitcast(FP8X4),
-                rhs_scale=h_s[:, cols(c, count)],
+                rhs=h_words(c, count)[:, j0 : j0 + width].bitcast(FP8X4),
+                rhs_scale=h_s[:, c * CHUNK + j0 : c * CHUNK + j0 + width],
                 start=True,
                 stop=True,
             )
@@ -180,68 +188,90 @@ def tile_list_modp_silu_none_kernel(
         for window in windows:
             for c0 in range(0, T, T // 2):
                 nc.vector.memset(window[:, c0 : c0 + T // 2], 0.0)
-        wd_s = sbuf("wd_s", [P, N // 4], I32)
-        nc.vector.memset(wd_s[:], 0)
+        def reorder_words(a, raw):
+            nc.vector.tensor_copy(
+                out=wu_w[:, a, :].rearrange("p (t m i) -> p m t i", t=PACK, i=LINE),
+                in_=raw.rearrange("p (m i t) -> p m t i", t=PACK, i=LINE),
+            )
+
+        def zero_on_gpsimd(name, offset):
+            window = after_words.tile([P, T], F32, name=name, offset=offset, align_bytes=ALIGN)
+            for c0 in range(0, T, T // 4):
+                nc.gpsimd.memset(window[:, c0 : c0 + T // 4], 0.0)
+            windows.append(window)
+
+        reorder_words(0, wu_raw0)
+        sm_t = after_words.tile([P, PACK], F32, name="sm_t", offset=sm_at, align_bytes=ALIGN)
+        wd_s = after_words.tile([P, N // 4], I32, name="wd_s", offset=wd_s_at, align_bytes=ALIGN)
+        nc.sync.dma_start(out=sm_t[:], in_=sm.rearrange("(p t) -> p t", t=PACK))
+        zero_on_gpsimd("window2", 0)
+        nc.gpsimd.memset(wd_s[:], 0)
+        zero_on_gpsimd("window3", window3_at)
         for q in range(QUADRANTS):
             nc.sync.dma_start(out=wd_s[32 * q : 32 * q + 4, :], in_=wd_scales[0, 4 * q : 4 * q + 4, :].bitcast(I32))
-        nc.vector.tensor_copy(
-            out=wu_w[:].rearrange("p a (t m i) -> p a m t i", t=PACK, i=LINE),
-            in_=wu_raw[:].rearrange("p a (m i t) -> p a m t i", t=PACK, i=LINE),
-        )
-        windows.append(reused.tile([P, T], F32, name="window2", offset=4 * T, align_bytes=ALIGN))
-        for c0 in range(0, T, T // 4):
-            nc.gpsimd.memset(windows[2][:, c0 : c0 + T // 4], 0.0)
         v_s = sbuf("v_s", [P, J], U8)
         nc.vector.tensor_copy(v_s[:], tab_s[:].bitcast(U8).indirect(offsets[:]))
         nc.vector.tensor_copy(
             out=wu_s[:].rearrange("p (t m) -> p t m", t=PACK),
             in_=wu_s_raw[:].bitcast(U8).rearrange("p (m t) -> p t m", t=PACK),
         )
-        windows.append(after_scales.tile([P, T], F32, name="window3", offset=wgo_at + 4 * J, align_bytes=ALIGN))
-        for c0 in range(0, T, T // 4):
-            nc.gpsimd.memset(windows[3][:, c0 : c0 + T // 4], 0.0)
         gather_words(0, 0)
-        gather_words(0, 1, 1, after_scales.tile([P, CHUNK], U32, name="v_w0_1", offset=0, align_bytes=ALIGN))
+        gather_words(0, 1)
+        reorder_words(1, wu_raw1[:])
+        gather_words(0, 2, 2)
         wd_w = after_scales.tile([P, N // 2], I32, name="wd_w", offset=wd_at, align_bytes=ALIGN)
         wgo_t = after_scales.tile([P, J], F32, name="wgo_t", offset=wgo_at, align_bytes=ALIGN)
         nc.sync.dma_start(out=wd_w[:], in_=wd_words[0].bitcast(I32))
         nc.sync.dma_start(out=wgo_t[:], in_=wgo)
         gather_words(1, 0)
-        gather_words(1, 1)
-        gather_words(1, 2, 2)
+        gather_words(1, 1, 2)
 
         first = up_banks([P, PACK, HALF], (0, 1))
         for b in range(2):
             up_pass(0, first[b], range(PACK), 0, b * HALF, HALF, True)
-        h0 = sbuf("h0", [P, CHUNK, PACK], BF16)
+        second = up_banks([P, 2, CHUNK], (2, 3))
+        for b in range(2):
+            up_pass(0, second[b], (2 * b, 2 * b + 1), 1, 0, CHUNK, True)
+        halves = []
         for b in range(2):
             up_pass(1, first[b], range(PACK), 0, b * HALF, HALF, False)
             act = sbuf("act0_%d" % b, [P, HALF, PACK], F32)
+            half = sbuf("h0_%d" % b, [P, HALF, PACK], BF16)[:]
             nc.scalar.activation(out=act[:], in_=first[b][:].rearrange("p t j -> p j t"), func=ACT.Silu)
-            nc.vector.tensor_tensor(
-                h0[:, b * HALF : (b + 1) * HALF, :], act[:], sm_t[:].unsqueeze(1).to_broadcast([P, HALF, PACK]), MULT
+            nc.vector.tensor_tensor(half, act[:], sm_t[:].unsqueeze(1).to_broadcast([P, HALF, PACK]), MULT)
+            halves.append(half)
+        for b in range(2):
+            nc.vector.quantize_mx(
+                out=h_first[:, b * HALF : (b + 1) * HALF].bitcast(FP8X4),
+                scales=h_s[:, b * HALF : (b + 1) * HALF],
+                in_=halves[b].rearrange("p j t -> p (j t)"),
             )
-        quantize(0, h0)
-        gather_words(0, 2, 2, sbuf("v_w0_2", [P, 2 * CHUNK], U32, "h0"))
+        gather_words(1, 3, 1, sbuf("v_w1_3", [P, CHUNK], U32, "h0_1"))
 
-        act = silu(1, up(1, (2, 3), 1))
-        sums = [down(n, 0, 4 + n) for n in range(ROW_TILES)]
-        for n in range(3):
+        for b in range(2):
+            up_pass(1, second[b], (2 * b, 2 * b + 1), 1, 0, CHUNK, False)
+        act = silu(1, second)
+        y_first = sbuf("y_first", [P, CHUNK], F32)
+        for b in range(2):
+            nc.scalar.copy(out=y_first[:, b * HALF : (b + 1) * HALF], in_=down(0, 0, (0, 4)[b], 1, b * HALF, HALF)[:])
+        place(windows[0], y_first[:], 0, 1)
+        sums = [None] + [down(n, 0, 4 + n) for n in range(1, ROW_TILES)]
+        for n in range(1, 3):
             copy_and_place(n, 0, sums[n])
         quantize(1, weave(1, scale(1, act, "h_first")))
         copy_and_place(3, 0, sums[3], 1, "h_first")
-        act = silu(2, up(2, (0, 1), 0))
+        act = silu(2, up(2, (4, 5), 1))
         for n in range(3):
-            copy_and_place(n, 1, down(n, 1, 4 + n))
+            copy_and_place(n, 1, down(n, 1, n))
         quantize(2, weave(2, scale(2, act, "planes2")))
-        copy_and_place(3, 1, down(3, 1, 7), 1, "planes2")
-        by_slice = scale(3, silu(3, up(3, (2, 3), 0)), "planes3")
-        copy_and_place(0, 2, down(0, 2, 4))
+        copy_and_place(3, 1, down(3, 1, 3), 1, "planes2")
+        by_slice = scale(3, silu(3, up(3, (6, 7), 1)), "planes3")
+        copy_and_place(0, 2, down(0, 2, 0))
         quantize(3, weave(3, by_slice))
-        copy_and_place(1, 2, down(1, 2, 5), 1, "planes3")
+        copy_and_place(1, 2, down(1, 2, 1), 1, "planes3")
         for n in range(2):
-            copy_and_place(n, 3, down(n, 3, n))
+            copy_and_place(n, 3, down(n, 3, 2 + n))
             store(n, windows[n])
         for n in range(2, 4):
-            copy_and_place(n, 2, down(n, 2, 4 + n, 2), 2)
+            copy_and_place(n, 2, down(n, 2, 2 + n, 2), 2)
             store(n, windows[n])

@@ -48,11 +48,10 @@ def tile_list_modp_silu_none_kernel(
         tab_s = sbuf("tab_s", [P, T // 4], I32)
         sm_at = 4 * T
         wd_s_at = sm_at + ALIGN
-        window3_at = wd_s_at + N
-        raw0_at = sm_at - 4 * R
-        wu_raw0 = after_words.tile(
-            [P, (window3_at + ALIGN - raw0_at) // 4], I32, name="wu_raw0", offset=raw0_at, align_bytes=ALIGN
-        )[:, :R]
+        raw_at = sm_at - 4 * PASSES * R
+        wu_raw = after_words.tile(
+            [P, (wd_s_at + ALIGN - raw_at) // 4], I32, name="wu_raw", offset=raw_at, align_bytes=ALIGN
+        )[:, : PASSES * R].rearrange("p (a r) -> p a r", a=PASSES)
         wu_w = sbuf("wu_w", [P, PASSES, R], I32)
         wu_s = sbuf("wu_s", [P, R], U8)
         h_first = sbuf("h_first", [P, CHUNK], U32)
@@ -60,19 +59,19 @@ def tile_list_modp_silu_none_kernel(
         h_s = sbuf("h_s", [P, J], U8)
         windows = [sbuf("window%d" % n, [P, T], F32) for n in range(2)]
         zeros = reused.tile([P, R // 4], I32, name="zeros", offset=0, align_bytes=ALIGN)
-        wd_at = 8 * CHUNK
+        wd_at = 4 * CHUNK
         wgo_at = wd_at + 2 * N
         spanning = after_scales.tile(
-            [P, (2 * N + 2 * ALIGN) // 4], I32, name="wu_s_raw", offset=wd_at - ALIGN, align_bytes=ALIGN
+            [P, (2 * N + 4 * J + 2 * ALIGN) // 4], I32, name="wu_s_raw", offset=wd_at - ALIGN, align_bytes=ALIGN
         )
         wu_s_raw = spanning[:, : R // 4]
         warm = sbuf("warm", [P, 1], F32)
         warm_out = sbuf("warm_out", [P, 1], F32, "tab_w1")
 
-        nc.vector.memset(tab_s[:], 0)
         nc.vector.memset(zeros[:], 0)
-        nc.vector.memset(warm[:], 0.0)
+        nc.vector.memset(tab_s[:], 0)
         nc.vector.tensor_copy(wu_s_raw[:], zeros[:])
+        nc.vector.memset(warm[:], 0.0)
         nc.scalar.activation(out=warm_out[:], in_=warm[:], func=ACT.Silu)
 
         tab_w = [reused.tile([P, T], I32, name="tab_w0", offset=0, align_bytes=ALIGN), sbuf("tab_w1", [P, T], I32)]
@@ -86,13 +85,11 @@ def tile_list_modp_silu_none_kernel(
                     out=tile[32 * q : 32 * q + 4 * PASSES, :], in_=scales[:, 4 * q : 4 * q + 4, :].bitcast(I32)
                 )
 
+        nc.sync.dma_start(out=wu_raw, in_=wu_words.rearrange("a p r i -> p a (r i)").bitcast(I32))
         nc.sync.dma_start(offsets[:], offs)
-        nc.sync.dma_start(out=wu_raw0, in_=wu_words[0].rearrange("p r i -> p (r i)").bitcast(I32))
         load_scales(tab_s, tab_scales)
-        load_scales(wu_s_raw, wu_scales)
         load_table(0)
-        wu_raw1 = sbuf("wu_raw1", [P, R], I32, "warm")
-        nc.sync.dma_start(out=wu_raw1[:], in_=wu_words[1].rearrange("p r i -> p (r i)").bitcast(I32))
+        load_scales(wu_s_raw, wu_scales)
         load_table(1)
 
         def cols(c, count=1):
@@ -138,9 +135,11 @@ def tile_list_modp_silu_none_kernel(
                 nc.scalar.activation(out=act[:, 2 * b : 2 * b + 2, :], in_=banks[b][:], func=ACT.Silu)
             return act
 
-        def scale(c, act, slices_tag):
-            by_slice = sbuf("planes%d" % c, [P, PACK, CHUNK], BF16, slices_tag)
-            for t in range(PACK):
+        def slices_tile(c, tag):
+            return sbuf("planes%d" % c, [P, PACK, CHUNK], BF16, tag)
+
+        def scale(by_slice, act, slices=range(PACK)):
+            for t in slices:
                 nc.scalar.activation(out=by_slice[:, t, :], in_=act[:, t, :], func=ACT.Copy, scale=sm_t[:, t : t + 1])
             return by_slice
 
@@ -188,50 +187,42 @@ def tile_list_modp_silu_none_kernel(
         for window in windows:
             for c0 in range(0, T, T // 2):
                 nc.vector.memset(window[:, c0 : c0 + T // 2], 0.0)
-        def reorder_words(a, raw):
-            nc.vector.tensor_copy(
-                out=wu_w[:, a, :].rearrange("p (t m i) -> p m t i", t=PACK, i=LINE),
-                in_=raw.rearrange("p (m i t) -> p m t i", t=PACK, i=LINE),
-            )
-
-        def zero_on_gpsimd(name, offset):
-            window = after_words.tile([P, T], F32, name=name, offset=offset, align_bytes=ALIGN)
+        def zero_on_gpsimd(window):
             for c0 in range(0, T, T // 4):
                 nc.gpsimd.memset(window[:, c0 : c0 + T // 4], 0.0)
             windows.append(window)
 
-        reorder_words(0, wu_raw0)
+        nc.vector.tensor_copy(
+            out=wu_w[:].rearrange("p a (t m i) -> p a m t i", t=PACK, i=LINE),
+            in_=wu_raw.rearrange("p a (m i t) -> p a m t i", t=PACK, i=LINE),
+        )
         sm_t = after_words.tile([P, PACK], F32, name="sm_t", offset=sm_at, align_bytes=ALIGN)
         wd_s = after_words.tile([P, N // 4], I32, name="wd_s", offset=wd_s_at, align_bytes=ALIGN)
         nc.sync.dma_start(out=sm_t[:], in_=sm.rearrange("(p t) -> p t", t=PACK))
-        zero_on_gpsimd("window2", 0)
+        zero_on_gpsimd(after_words.tile([P, T], F32, name="window2", offset=0, align_bytes=ALIGN))
         nc.gpsimd.memset(wd_s[:], 0)
-        zero_on_gpsimd("window3", window3_at)
         for q in range(QUADRANTS):
             nc.sync.dma_start(out=wd_s[32 * q : 32 * q + 4, :], in_=wd_scales[0, 4 * q : 4 * q + 4, :].bitcast(I32))
         v_s = sbuf("v_s", [P, J], U8)
         nc.vector.tensor_copy(v_s[:], tab_s[:].bitcast(U8).indirect(offsets[:]))
+        gather_words(0, 0)
         nc.vector.tensor_copy(
             out=wu_s[:].rearrange("p (t m) -> p t m", t=PACK),
             in_=wu_s_raw[:].bitcast(U8).rearrange("p (m t) -> p t m", t=PACK),
         )
-        gather_words(0, 0)
-        gather_words(0, 1)
-        reorder_words(1, wu_raw1[:])
-        gather_words(0, 2, 2)
+        zero_on_gpsimd(after_scales.tile([P, T], F32, name="window3", offset=wgo_at + 4 * J, align_bytes=ALIGN))
+        gather_words(0, 1, 1, after_scales.tile([P, CHUNK], U32, name="v_w0_1", offset=0, align_bytes=ALIGN))
         wd_w = after_scales.tile([P, N // 2], I32, name="wd_w", offset=wd_at, align_bytes=ALIGN)
         wgo_t = after_scales.tile([P, J], F32, name="wgo_t", offset=wgo_at, align_bytes=ALIGN)
         nc.sync.dma_start(out=wd_w[:], in_=wd_words[0].bitcast(I32))
         nc.sync.dma_start(out=wgo_t[:], in_=wgo)
         gather_words(1, 0)
-        gather_words(1, 1, 2)
+        gather_words(1, 1)
+        gather_words(1, 2, 2)
 
         first = up_banks([P, PACK, HALF], (0, 1))
         for b in range(2):
             up_pass(0, first[b], range(PACK), 0, b * HALF, HALF, True)
-        second = up_banks([P, 2, CHUNK], (2, 3))
-        for b in range(2):
-            up_pass(0, second[b], (2 * b, 2 * b + 1), 1, 0, CHUNK, True)
         halves = []
         for b in range(2):
             up_pass(1, first[b], range(PACK), 0, b * HALF, HALF, False)
@@ -246,11 +237,9 @@ def tile_list_modp_silu_none_kernel(
                 scales=h_s[:, b * HALF : (b + 1) * HALF],
                 in_=halves[b].rearrange("p j t -> p (j t)"),
             )
-        gather_words(1, 3, 1, sbuf("v_w1_3", [P, CHUNK], U32, "h0_1"))
+        gather_words(0, 2, 2, sbuf("v_w0_2", [P, 2 * CHUNK], U32, "h0_1"))
 
-        for b in range(2):
-            up_pass(1, second[b], (2 * b, 2 * b + 1), 1, 0, CHUNK, False)
-        act = silu(1, second)
+        act = silu(1, up(1, (2, 3), 1))
         y_first = sbuf("y_first", [P, CHUNK], F32)
         for b in range(2):
             nc.scalar.copy(out=y_first[:, b * HALF : (b + 1) * HALF], in_=down(0, 0, (0, 4)[b], 1, b * HALF, HALF)[:])
@@ -258,14 +247,15 @@ def tile_list_modp_silu_none_kernel(
         sums = [None] + [down(n, 0, 4 + n) for n in range(1, ROW_TILES)]
         for n in range(1, 3):
             copy_and_place(n, 0, sums[n])
-        quantize(1, weave(1, scale(1, act, "h_first")))
+        quantize(1, weave(1, scale(slices_tile(1, "h_first"), act)))
         copy_and_place(3, 0, sums[3], 1, "h_first")
-        act = silu(2, up(2, (4, 5), 1))
+        act = silu(2, up(2, (4, 5), 0))
+        by_slice = scale(slices_tile(2, "planes2"), act, (0, 1))
         for n in range(3):
             copy_and_place(n, 1, down(n, 1, n))
-        quantize(2, weave(2, scale(2, act, "planes2")))
+        quantize(2, weave(2, scale(by_slice, act, (2, 3))))
         copy_and_place(3, 1, down(3, 1, 3), 1, "planes2")
-        by_slice = scale(3, silu(3, up(3, (6, 7), 1)), "planes3")
+        by_slice = scale(slices_tile(3, "planes3"), silu(3, up(3, (6, 7), 0)))
         copy_and_place(0, 2, down(0, 2, 0))
         quantize(3, weave(3, by_slice))
         copy_and_place(1, 2, down(1, 2, 1), 1, "planes3")
@@ -274,4 +264,6 @@ def tile_list_modp_silu_none_kernel(
             store(n, windows[n])
         for n in range(2, 4):
             copy_and_place(n, 2, down(n, 2, 2 + n, 2), 2)
-            store(n, windows[n])
+        store(2, windows[2])
+        nc.sync.dma_start(out=out[3 * P :, : T // 2], in_=windows[3][:, : T // 2])
+        nc.scalar.dma_start(out=out[3 * P :, T // 2 :], in_=windows[3][:, T // 2 :])

@@ -264,6 +264,4 @@ def tile_list_modp_silu_none_kernel(
             store(n, windows[n])
         for n in range(2, 4):
             copy_and_place(n, 2, down(n, 2, 2 + n, 2), 2)
-        store(2, windows[2])
-        nc.sync.dma_start(out=out[3 * P :, : T // 2], in_=windows[3][:, : T // 2])
-        nc.scalar.dma_start(out=out[3 * P :, T // 2 :], in_=windows[3][:, T // 2 :])
+            store(n, windows[n])

@@ -48,33 +48,45 @@ def tile_list_modp_silu_none_kernel(
         tab_s = sbuf("tab_s", [P, T // 4], I32)
         sm_at = 4 * T
         wd_s_at = sm_at + ALIGN
-        raw_at = sm_at - 4 * PASSES * R
-        wu_raw = after_words.tile(
-            [P, (wd_s_at + ALIGN - raw_at) // 4], I32, name="wu_raw", offset=raw_at, align_bytes=ALIGN
-        )[:, : PASSES * R].rearrange("p (a r) -> p a r", a=PASSES)
+        raw_at = sm_at - 4 * R
+        wu_raw0 = after_words.tile(
+            [P, (wd_s_at + ALIGN - raw_at) // 4], I32, name="wu_raw0", offset=raw_at, align_bytes=ALIGN
+        )[:, :R]
         wu_w = sbuf("wu_w", [P, PASSES, R], I32)
         wu_s = sbuf("wu_s", [P, R], U8)
         h_first = sbuf("h_first", [P, CHUNK], U32)
         h_rest = sbuf("h_rest", [P, J - CHUNK], U32)
         h_s = sbuf("h_s", [P, J], U8)
-        windows = [sbuf("window%d" % n, [P, T], F32) for n in range(2)]
-        zeros = reused.tile([P, R // 4], I32, name="zeros", offset=0, align_bytes=ALIGN)
-        wd_at = 4 * CHUNK
+        windows = [sbuf("window%d" % n, [P, T], F32) for n in range(3)]
+        raw1_at = 4 * T
+        tab1_at = raw1_at + 4 * R
+        zeros = reused.tile(
+            [P, (4 * R + 2 * ALIGN) // 4], I32, name="zeros", offset=raw1_at - ALIGN, align_bytes=ALIGN
+        )[:, : R // 4]
+        wd_at = 4 * (J - CHUNK)
         wgo_at = wd_at + 2 * N
         spanning = after_scales.tile(
-            [P, (2 * N + 4 * J + 2 * ALIGN) // 4], I32, name="wu_s_raw", offset=wd_at - ALIGN, align_bytes=ALIGN
+            [P, (8 * CHUNK + 2 * N + 2 * ALIGN) // 4], I32, name="wu_s_raw", offset=4 * CHUNK - ALIGN, align_bytes=ALIGN
         )
         wu_s_raw = spanning[:, : R // 4]
-        warm = sbuf("warm", [P, 1], F32)
-        warm_out = sbuf("warm_out", [P, 1], F32, "tab_w1")
 
-        nc.vector.memset(zeros[:], 0)
         nc.vector.memset(tab_s[:], 0)
-        nc.vector.tensor_copy(wu_s_raw[:], zeros[:])
-        nc.vector.memset(warm[:], 0.0)
-        nc.scalar.activation(out=warm_out[:], in_=warm[:], func=ACT.Silu)
+        nc.vector.memset(zeros, 0)
+        nc.vector.tensor_copy(wu_s_raw[:], zeros)
 
-        tab_w = [reused.tile([P, T], I32, name="tab_w0", offset=0, align_bytes=ALIGN), sbuf("tab_w1", [P, T], I32)]
+        tab_w = [
+            reused.tile([P, T], I32, name="tab_w%d" % a, offset=(0, tab1_at)[a], align_bytes=ALIGN) for a in range(2)
+        ]
+        wu_raw = [wu_raw0, reused.tile([P, R], I32, name="wu_raw1", offset=raw1_at, align_bytes=ALIGN)[:]]
+
+        def load_wu(a):
+            nc.sync.dma_start(out=wu_raw[a], in_=wu_words[a].rearrange("p r i -> p (r i)").bitcast(I32))
+
+        def reorder_wu(a):
+            nc.scalar.copy(
+                out=wu_w[:, a, :].bitcast(U32).rearrange("p (t m i) -> p m t i", t=PACK, i=LINE),
+                in_=wu_raw[a].bitcast(U32).rearrange("p (m i t) -> p m t i", t=PACK, i=LINE),
+            )
 
         def load_table(a):
             nc.sync.dma_start(out=tab_w[a][:], in_=tab_words[a].rearrange("p t i -> p (t i)").bitcast(I32))
@@ -85,11 +97,12 @@ def tile_list_modp_silu_none_kernel(
                     out=tile[32 * q : 32 * q + 4 * PASSES, :], in_=scales[:, 4 * q : 4 * q + 4, :].bitcast(I32)
                 )
 
-        nc.sync.dma_start(out=wu_raw, in_=wu_words.rearrange("a p r i -> p a (r i)").bitcast(I32))
+        load_wu(0)
         nc.sync.dma_start(offsets[:], offs)
         load_scales(tab_s, tab_scales)
         load_table(0)
         load_scales(wu_s_raw, wu_scales)
+        load_wu(1)
         load_table(1)
 
         def cols(c, count=1):
@@ -100,23 +113,28 @@ def tile_list_modp_silu_none_kernel(
 
         v_w = {}
 
-        def gather_words(a, c, count=1, tile=None):
+        def gather_words(a, first, count, tile=None):
             if tile is None:
-                tile = sbuf("v_w%d_%d" % (a, c), [P, count * CHUNK], U32)
-            nc.vector.tensor_copy(tile[:], tab_w[a][:].bitcast(U32).indirect(listed(c, count)))
-            for i in range(count):
-                v_w[a, c + i] = tile[:, i * CHUNK : (i + 1) * CHUNK]
+                tile = sbuf("v_w%d_%d" % (a, first), [P, count * HALF], U32)
+            picks = offsets[:, first * HALF // LIST_ROWS : (first + count) * HALF // LIST_ROWS]
+            nc.vector.tensor_copy(tile[:], tab_w[a][:].bitcast(U32).indirect(picks))
+            for c in range(first // 2, (first + count + 1) // 2):
+                lo, hi = max(first, 2 * c), min(first + count, 2 * c + 2)
+                run = ((lo - 2 * c) * HALF, tile[:, (lo - first) * HALF : (hi - first) * HALF])
+                v_w.setdefault((a, c), []).append(run)
 
-        def up_pass(a, bank, slices, c, j0, width, opening):
-            for i, t in enumerate(slices):
+        def up_pass(a, bank, slices, c, opening, runs=None, at=0):
+            steps = [(i, t, j0, words) for i, t in enumerate(slices) for j0, words in (runs or v_w[a, c])]
+            for step, (i, t, j0, words) in enumerate(steps):
+                width = words.shape[1]
                 nc.tensor.matmul_mx(
-                    out=bank[:, i, :],
+                    out=bank[:, i, j0 - at : j0 - at + width],
                     lhsT=wu_w[:, a, t * P : (t + 1) * P].bitcast(FP8X4),
                     lhsT_scale=wu_s[4 * a :, t * P : (t + 1) * P],
-                    rhs=v_w[a, c][:, j0 : j0 + width].bitcast(FP8X4),
+                    rhs=words.bitcast(FP8X4),
                     rhs_scale=v_s[4 * a :, c * CHUNK + j0 : c * CHUNK + j0 + width],
-                    start=(opening and i == 0),
-                    stop=(not opening and i == len(slices) - 1),
+                    start=(opening and step == 0),
+                    stop=(not opening and step == len(steps) - 1),
                 )
 
         def up_banks(shape, numbers):
@@ -126,7 +144,7 @@ def tile_list_modp_silu_none_kernel(
             banks = up_banks([P, 2, CHUNK], numbers)
             for a in (opening_pass, 1 - opening_pass):
                 for b in range(2):
-                    up_pass(a, banks[b], (2 * b, 2 * b + 1), c, 0, CHUNK, a == opening_pass)
+                    up_pass(a, banks[b], (2 * b, 2 * b + 1), c, a == opening_pass)
             return banks
 
         def silu(c, banks):
@@ -192,44 +210,48 @@ def tile_list_modp_silu_none_kernel(
                 nc.gpsimd.memset(window[:, c0 : c0 + T // 4], 0.0)
             windows.append(window)
 
-        nc.vector.tensor_copy(
-            out=wu_w[:].rearrange("p a (t m i) -> p a m t i", t=PACK, i=LINE),
-            in_=wu_raw.rearrange("p a (m i t) -> p a m t i", t=PACK, i=LINE),
-        )
+        for a in range(PASSES):
+            reorder_wu(a)
         sm_t = after_words.tile([P, PACK], F32, name="sm_t", offset=sm_at, align_bytes=ALIGN)
         wd_s = after_words.tile([P, N // 4], I32, name="wd_s", offset=wd_s_at, align_bytes=ALIGN)
         nc.sync.dma_start(out=sm_t[:], in_=sm.rearrange("(p t) -> p t", t=PACK))
-        zero_on_gpsimd(after_words.tile([P, T], F32, name="window2", offset=0, align_bytes=ALIGN))
+        zero_on_gpsimd(after_words.tile([P, T], F32, name="window3", offset=0, align_bytes=ALIGN))
         nc.gpsimd.memset(wd_s[:], 0)
         for q in range(QUADRANTS):
             nc.sync.dma_start(out=wd_s[32 * q : 32 * q + 4, :], in_=wd_scales[0, 4 * q : 4 * q + 4, :].bitcast(I32))
         v_s = sbuf("v_s", [P, J], U8)
         nc.vector.tensor_copy(v_s[:], tab_s[:].bitcast(U8).indirect(offsets[:]))
-        gather_words(0, 0)
+        gather_words(0, 0, 2)
+        gather_words(0, 2, 2)
         nc.vector.tensor_copy(
             out=wu_s[:].rearrange("p (t m) -> p t m", t=PACK),
             in_=wu_s_raw[:].bitcast(U8).rearrange("p (m t) -> p t m", t=PACK),
         )
-        zero_on_gpsimd(after_scales.tile([P, T], F32, name="window3", offset=wgo_at + 4 * J, align_bytes=ALIGN))
-        gather_words(0, 1, 1, after_scales.tile([P, CHUNK], U32, name="v_w0_1", offset=0, align_bytes=ALIGN))
+        gather_words(0, 4, 4, reused.tile([P, 4 * HALF], U32, name="v_w0_4", offset=raw1_at, align_bytes=ALIGN))
         wd_w = after_scales.tile([P, N // 2], I32, name="wd_w", offset=wd_at, align_bytes=ALIGN)
         wgo_t = after_scales.tile([P, J], F32, name="wgo_t", offset=wgo_at, align_bytes=ALIGN)
         nc.sync.dma_start(out=wd_w[:], in_=wd_words[0].bitcast(I32))
         nc.sync.dma_start(out=wgo_t[:], in_=wgo)
-        gather_words(1, 0)
-        gather_words(1, 1)
+        gather_words(1, 0, 1)
+        gather_words(1, 1, 1)
         gather_words(1, 2, 2)
+        gather_words(1, 4, 2)
 
         first = up_banks([P, PACK, HALF], (0, 1))
         for b in range(2):
-            up_pass(0, first[b], range(PACK), 0, b * HALF, HALF, True)
+            words = v_w[0, 0][0][1][:, b * HALF : (b + 1) * HALF]
+            up_pass(0, first[b], range(PACK), 0, True, [(b * HALF, words)], b * HALF)
         halves = []
         for b in range(2):
-            up_pass(1, first[b], range(PACK), 0, b * HALF, HALF, False)
-            act = sbuf("act0_%d" % b, [P, HALF, PACK], F32)
+            up_pass(1, first[b], range(PACK), 0, False, [v_w[1, 0][b]], b * HALF)
             half = sbuf("h0_%d" % b, [P, HALF, PACK], BF16)[:]
-            nc.scalar.activation(out=act[:], in_=first[b][:].rearrange("p t j -> p j t"), func=ACT.Silu)
-            nc.vector.tensor_tensor(half, act[:], sm_t[:].unsqueeze(1).to_broadcast([P, HALF, PACK]), MULT)
+            for q in range(2):
+                part = slice(q * HALF // 2, (q + 1) * HALF // 2)
+                act = sbuf("act0_%d_%d" % (b, q), [P, HALF // 2, PACK], F32)
+                nc.scalar.activation(out=act[:], in_=first[b][:, :, part].rearrange("p t j -> p j t"), func=ACT.Silu)
+                nc.vector.tensor_tensor(
+                    half[:, part, :], act[:], sm_t[:].unsqueeze(1).to_broadcast([P, HALF // 2, PACK]), MULT
+                )
             halves.append(half)
         for b in range(2):
             nc.vector.quantize_mx(
@@ -237,7 +259,7 @@ def tile_list_modp_silu_none_kernel(
                 scales=h_s[:, b * HALF : (b + 1) * HALF],
                 in_=halves[b].rearrange("p j t -> p (j t)"),
             )
-        gather_words(0, 2, 2, sbuf("v_w0_2", [P, 2 * CHUNK], U32, "h0_1"))
+        gather_words(1, 6, 2, sbuf("v_w1_6", [P, 2 * HALF], U32, "act0_1_1"))
 
         act = silu(1, up(1, (2, 3), 1))
         y_first = sbuf("y_first", [P, CHUNK], F32)

@@ -21,11 +21,12 @@ PACK = 4
 PASSES = K // (P * PACK)
 CHUNK = 256
 HALF = CHUNK // 2
-CHUNKS = J // CHUNK
+QUARTER = CHUNK // 4
 ROW_TILES = N // P
-WINDOWS = ROW_TILES
+ON_VECTOR = 3
 LIST_ROWS = 16
 QUADRANTS = 4
+WORD = 4
 LINE = 4
 ALIGN = 64
 
@@ -36,7 +37,7 @@ def tile_list_modp_silu_none_kernel(
     nc = tc.nc
     with ExitStack() as ctx:
         keep = ctx.enter_context(tc.tile_pool(name="keep", bufs=1))
-        reused = ctx.enter_context(tc.tile_pool(name="reused", bufs=1))
+        after_zeros = ctx.enter_context(tc.tile_pool(name="after_zeros", bufs=1))
         after_scales = ctx.enter_context(tc.tile_pool(name="after_scales", bufs=1))
         after_words = ctx.enter_context(tc.tile_pool(name="after_words", bufs=1))
         psum = ctx.enter_context(tc.psum_pool(name="psum", bufs=1))
@@ -44,52 +45,38 @@ def tile_list_modp_silu_none_kernel(
         def sbuf(name, shape, dtype, tag=None):
             return keep.tile(shape, dtype, name=name, tag=tag or name, align_bytes=ALIGN)
 
+        def placed(pool, name, columns, dtype, at):
+            return pool.tile([P, columns], dtype, name=name, offset=at, align_bytes=ALIGN)
+
+        def spanning(pool, name, columns, start, stop):
+            return placed(pool, name, (stop - start) // WORD, I32, start)[:, :columns]
+
         offsets = keep.tile([P, J // LIST_ROWS], U16, name="offsets")
-        tab_s = sbuf("tab_s", [P, T // 4], I32)
-        sm_at = 4 * T
-        wd_s_at = sm_at + ALIGN
-        raw_at = sm_at - 4 * R
-        wu_raw0 = after_words.tile(
-            [P, (wd_s_at + ALIGN - raw_at) // 4], I32, name="wu_raw0", offset=raw_at, align_bytes=ALIGN
-        )[:, :R]
+        tab_s = sbuf("tab_s", [P, T // WORD], I32)
         wu_w = sbuf("wu_w", [P, PASSES, R], I32)
         wu_s = sbuf("wu_s", [P, R], U8)
         h_first = sbuf("h_first", [P, CHUNK], U32)
         h_rest = sbuf("h_rest", [P, J - CHUNK], U32)
         h_s = sbuf("h_s", [P, J], U8)
-        windows = [sbuf("window%d" % n, [P, T], F32) for n in range(3)]
-        raw1_at = 4 * T
-        tab1_at = raw1_at + 4 * R
-        zeros = reused.tile(
-            [P, (4 * R + 2 * ALIGN) // 4], I32, name="zeros", offset=raw1_at - ALIGN, align_bytes=ALIGN
-        )[:, : R // 4]
-        wd_at = 4 * (J - CHUNK)
-        wgo_at = wd_at + 2 * N
-        spanning = after_scales.tile(
-            [P, (8 * CHUNK + 2 * N + 2 * ALIGN) // 4], I32, name="wu_s_raw", offset=4 * CHUNK - ALIGN, align_bytes=ALIGN
-        )
-        wu_s_raw = spanning[:, : R // 4]
+        windows = [sbuf("window%d" % n, [P, T], F32) for n in range(ON_VECTOR)]
+        sm_at = WORD * T
+        wd_s_at = sm_at + ALIGN
+        wu_raw0 = spanning(after_words, "wu_raw0", R, sm_at - WORD * R, wd_s_at + ALIGN)
+        wu_raw1_at = WORD * T
+        tab1_at = wu_raw1_at + WORD * R
+        zeros = spanning(after_zeros, "zeros", R // WORD, wu_raw1_at - ALIGN, tab1_at + ALIGN)
+        wgo_at = 2 * N
+        wu_s_raw = spanning(after_scales, "wu_s_raw", R // WORD, 0, wgo_at + ALIGN)
 
         nc.vector.memset(tab_s[:], 0)
         nc.vector.memset(zeros, 0)
-        nc.vector.tensor_copy(wu_s_raw[:], zeros)
+        nc.vector.tensor_copy(wu_s_raw, zeros)
 
-        tab_w = [
-            reused.tile([P, T], I32, name="tab_w%d" % a, offset=(0, tab1_at)[a], align_bytes=ALIGN) for a in range(2)
-        ]
-        wu_raw = [wu_raw0, reused.tile([P, R], I32, name="wu_raw1", offset=raw1_at, align_bytes=ALIGN)[:]]
+        tab_w = [placed(after_zeros, "tab_w%d" % a, T, I32, at) for a, at in enumerate((0, tab1_at))]
+        wu_raw = [wu_raw0, placed(after_zeros, "wu_raw1", R, I32, wu_raw1_at)[:]]
 
-        def load_wu(a):
-            nc.sync.dma_start(out=wu_raw[a], in_=wu_words[a].rearrange("p r i -> p (r i)").bitcast(I32))
-
-        def reorder_wu(a):
-            nc.scalar.copy(
-                out=wu_w[:, a, :].bitcast(U32).rearrange("p (t m i) -> p m t i", t=PACK, i=LINE),
-                in_=wu_raw[a].bitcast(U32).rearrange("p (m i t) -> p m t i", t=PACK, i=LINE),
-            )
-
-        def load_table(a):
-            nc.sync.dma_start(out=tab_w[a][:], in_=tab_words[a].rearrange("p t i -> p (t i)").bitcast(I32))
+        def load_words(tile, words):
+            nc.sync.dma_start(out=tile, in_=words.rearrange("p c i -> p (c i)").bitcast(I32))
 
         def load_scales(tile, scales):
             for q in range(QUADRANTS):
@@ -97,44 +84,43 @@ def tile_list_modp_silu_none_kernel(
                     out=tile[32 * q : 32 * q + 4 * PASSES, :], in_=scales[:, 4 * q : 4 * q + 4, :].bitcast(I32)
                 )
 
-        load_wu(0)
+        load_words(wu_raw[0], wu_words[0])
         nc.sync.dma_start(offsets[:], offs)
         load_scales(tab_s, tab_scales)
-        load_table(0)
+        load_words(tab_w[0][:], tab_words[0])
         load_scales(wu_s_raw, wu_scales)
-        load_wu(1)
-        load_table(1)
+        load_words(wu_raw[1], wu_words[1])
+        load_words(tab_w[1][:], tab_words[1])
 
         def cols(c, count=1):
             return slice(c * CHUNK, (c + count) * CHUNK)
 
-        def listed(c, count=1):
-            return offsets[:, c * CHUNK // LIST_ROWS : (c + count) * CHUNK // LIST_ROWS]
+        def listed(entries):
+            return offsets[:, entries.start // LIST_ROWS : entries.stop // LIST_ROWS]
+
+        def gather_words(a, entries, tile):
+            nc.vector.tensor_copy(tile[:], tab_w[a][:].bitcast(U32).indirect(listed(entries)))
+            return tile[:]
 
         v_w = {}
 
-        def gather_words(a, first, count, tile=None):
+        def gather_chunks(a, c, count=1, tile=None):
             if tile is None:
-                tile = sbuf("v_w%d_%d" % (a, first), [P, count * HALF], U32)
-            picks = offsets[:, first * HALF // LIST_ROWS : (first + count) * HALF // LIST_ROWS]
-            nc.vector.tensor_copy(tile[:], tab_w[a][:].bitcast(U32).indirect(picks))
-            for c in range(first // 2, (first + count + 1) // 2):
-                lo, hi = max(first, 2 * c), min(first + count, 2 * c + 2)
-                run = ((lo - 2 * c) * HALF, tile[:, (lo - first) * HALF : (hi - first) * HALF])
-                v_w.setdefault((a, c), []).append(run)
+                tile = sbuf("v_w%d_%d" % (a, c), [P, count * CHUNK], U32)
+            words = gather_words(a, cols(c, count), tile)
+            for i in range(count):
+                v_w[a, c + i] = words[:, cols(i)]
 
-        def up_pass(a, bank, slices, c, opening, runs=None, at=0):
-            steps = [(i, t, j0, words) for i, t in enumerate(slices) for j0, words in (runs or v_w[a, c])]
-            for step, (i, t, j0, words) in enumerate(steps):
-                width = words.shape[1]
+        def up_pass(a, bank, slices, words, entries, opening):
+            for i, t in enumerate(slices):
                 nc.tensor.matmul_mx(
-                    out=bank[:, i, j0 - at : j0 - at + width],
+                    out=bank[:, i, :],
                     lhsT=wu_w[:, a, t * P : (t + 1) * P].bitcast(FP8X4),
                     lhsT_scale=wu_s[4 * a :, t * P : (t + 1) * P],
                     rhs=words.bitcast(FP8X4),
-                    rhs_scale=v_s[4 * a :, c * CHUNK + j0 : c * CHUNK + j0 + width],
-                    start=(opening and step == 0),
-                    stop=(not opening and step == len(steps) - 1),
+                    rhs_scale=v_s[4 * a :, entries],
+                    start=(opening and i == 0),
+                    stop=(not opening and i == len(slices) - 1),
                 )
 
         def up_banks(shape, numbers):
@@ -144,7 +130,7 @@ def tile_list_modp_silu_none_kernel(
             banks = up_banks([P, 2, CHUNK], numbers)
             for a in (opening_pass, 1 - opening_pass):
                 for b in range(2):
-                    up_pass(a, banks[b], (2 * b, 2 * b + 1), c, a == opening_pass)
+                    up_pass(a, banks[b], (2 * b, 2 * b + 1), v_w[a, c], cols(c), a == opening_pass)
             return banks
 
         def silu(c, banks):
@@ -154,7 +140,7 @@ def tile_list_modp_silu_none_kernel(
             return act
 
         def slices_tile(c, tag):
-            return sbuf("planes%d" % c, [P, PACK, CHUNK], BF16, tag)
+            return sbuf("by_slice%d" % c, [P, PACK, CHUNK], BF16, tag)
 
         def scale(by_slice, act, slices=range(PACK)):
             for t in slices:
@@ -192,98 +178,100 @@ def tile_list_modp_silu_none_kernel(
             return bank
 
         def place(window, y, c, count):
-            nc.vector.tensor_tensor(window[:].indirect(listed(c, count)), y, wgo_t[:, cols(c, count)], MULT)
+            entries = cols(c, count)
+            nc.vector.tensor_tensor(window[:].indirect(listed(entries)), y, wgo_t[:, entries], MULT)
 
         def copy_and_place(n, c, bank, count=1, tag=None):
             y = sbuf("y%d_%d" % (n, c), [P, count * CHUNK], F32, tag)
             nc.scalar.copy(out=y[:], in_=bank[:])
             place(windows[n], y[:], c, count)
 
-        def store(n, window):
-            nc.sync.dma_start(out=out[n * P : (n + 1) * P, :], in_=window[:])
+        def store(n):
+            nc.sync.dma_start(out=out[n * P : (n + 1) * P, :], in_=windows[n][:])
 
         for window in windows:
             for c0 in range(0, T, T // 2):
                 nc.vector.memset(window[:, c0 : c0 + T // 2], 0.0)
-        def zero_on_gpsimd(window):
-            for c0 in range(0, T, T // 4):
-                nc.gpsimd.memset(window[:, c0 : c0 + T // 4], 0.0)
-            windows.append(window)
 
         for a in range(PASSES):
-            reorder_wu(a)
-        sm_t = after_words.tile([P, PACK], F32, name="sm_t", offset=sm_at, align_bytes=ALIGN)
-        wd_s = after_words.tile([P, N // 4], I32, name="wd_s", offset=wd_s_at, align_bytes=ALIGN)
+            nc.scalar.copy(
+                out=wu_w[:, a, :].bitcast(U32).rearrange("p (t m i) -> p m t i", t=PACK, i=LINE),
+                in_=wu_raw[a].bitcast(U32).rearrange("p (m i t) -> p m t i", t=PACK, i=LINE),
+            )
+        sm_t = placed(after_words, "sm_t", PACK, F32, sm_at)
+        wd_s = placed(after_words, "wd_s", N // WORD, I32, wd_s_at)
         nc.sync.dma_start(out=sm_t[:], in_=sm.rearrange("(p t) -> p t", t=PACK))
-        zero_on_gpsimd(after_words.tile([P, T], F32, name="window3", offset=0, align_bytes=ALIGN))
+        windows.append(placed(after_words, "last_window", T, F32, 0))
+        for c0 in range(0, T, T // 4):
+            nc.gpsimd.memset(windows[ON_VECTOR][:, c0 : c0 + T // 4], 0.0)
         nc.gpsimd.memset(wd_s[:], 0)
         for q in range(QUADRANTS):
             nc.sync.dma_start(out=wd_s[32 * q : 32 * q + 4, :], in_=wd_scales[0, 4 * q : 4 * q + 4, :].bitcast(I32))
+
         v_s = sbuf("v_s", [P, J], U8)
         nc.vector.tensor_copy(v_s[:], tab_s[:].bitcast(U8).indirect(offsets[:]))
-        gather_words(0, 0, 2)
-        gather_words(0, 2, 2)
+        gather_chunks(0, 0)
+        gather_chunks(0, 1)
         nc.vector.tensor_copy(
             out=wu_s[:].rearrange("p (t m) -> p t m", t=PACK),
-            in_=wu_s_raw[:].bitcast(U8).rearrange("p (m t) -> p t m", t=PACK),
+            in_=wu_s_raw.bitcast(U8).rearrange("p (m t) -> p t m", t=PACK),
         )
-        gather_words(0, 4, 4, reused.tile([P, 4 * HALF], U32, name="v_w0_4", offset=raw1_at, align_bytes=ALIGN))
-        wd_w = after_scales.tile([P, N // 2], I32, name="wd_w", offset=wd_at, align_bytes=ALIGN)
-        wgo_t = after_scales.tile([P, J], F32, name="wgo_t", offset=wgo_at, align_bytes=ALIGN)
+        gather_chunks(0, 2, 2, placed(after_zeros, "v_w0_2", 2 * CHUNK, U32, wu_raw1_at))
+        wd_w = placed(after_scales, "wd_w", wgo_at // WORD, I32, 0)
+        wgo_t = placed(after_scales, "wgo_t", J, F32, wgo_at)
         nc.sync.dma_start(out=wd_w[:], in_=wd_words[0].bitcast(I32))
         nc.sync.dma_start(out=wgo_t[:], in_=wgo)
-        gather_words(1, 0, 1)
-        gather_words(1, 1, 1)
-        gather_words(1, 2, 2)
-        gather_words(1, 4, 2)
+        halves = [slice(b * HALF, (b + 1) * HALF) for b in range(2)]
+        closing_words = [gather_words(1, halves[b], sbuf("v_half%d" % b, [P, HALF], U32)) for b in range(2)]
+        gather_chunks(1, 1)
+        gather_chunks(1, 2)
 
         first = up_banks([P, PACK, HALF], (0, 1))
         for b in range(2):
-            words = v_w[0, 0][0][1][:, b * HALF : (b + 1) * HALF]
-            up_pass(0, first[b], range(PACK), 0, True, [(b * HALF, words)], b * HALF)
-        halves = []
+            up_pass(0, first[b], range(PACK), v_w[0, 0][:, halves[b]], halves[b], True)
+        h_halves = []
         for b in range(2):
-            up_pass(1, first[b], range(PACK), 0, False, [v_w[1, 0][b]], b * HALF)
-            half = sbuf("h0_%d" % b, [P, HALF, PACK], BF16)[:]
+            up_pass(1, first[b], range(PACK), closing_words[b], halves[b], False)
+            h_half = sbuf("h0_%d" % b, [P, HALF, PACK], BF16)[:]
             for q in range(2):
-                part = slice(q * HALF // 2, (q + 1) * HALF // 2)
-                act = sbuf("act0_%d_%d" % (b, q), [P, HALF // 2, PACK], F32)
+                part = slice(q * QUARTER, (q + 1) * QUARTER)
+                act = sbuf("act0_%d" % (2 * b + q), [P, QUARTER, PACK], F32)
                 nc.scalar.activation(out=act[:], in_=first[b][:, :, part].rearrange("p t j -> p j t"), func=ACT.Silu)
                 nc.vector.tensor_tensor(
-                    half[:, part, :], act[:], sm_t[:].unsqueeze(1).to_broadcast([P, HALF // 2, PACK]), MULT
+                    h_half[:, part, :], act[:], sm_t[:].unsqueeze(1).to_broadcast([P, QUARTER, PACK]), MULT
                 )
-            halves.append(half)
+            h_halves.append(h_half)
         for b in range(2):
             nc.vector.quantize_mx(
-                out=h_first[:, b * HALF : (b + 1) * HALF].bitcast(FP8X4),
-                scales=h_s[:, b * HALF : (b + 1) * HALF],
-                in_=halves[b].rearrange("p j t -> p (j t)"),
+                out=h_first[:, halves[b]].bitcast(FP8X4),
+                scales=h_s[:, halves[b]],
+                in_=h_halves[b].rearrange("p j t -> p (j t)"),
             )
-        gather_words(1, 6, 2, sbuf("v_w1_6", [P, 2 * HALF], U32, "act0_1_1"))
+        gather_chunks(1, 3, 1, sbuf("v_w1_3", [P, CHUNK], U32, "act0_3"))
 
         act = silu(1, up(1, (2, 3), 1))
         y_first = sbuf("y_first", [P, CHUNK], F32)
-        for b in range(2):
-            nc.scalar.copy(out=y_first[:, b * HALF : (b + 1) * HALF], in_=down(0, 0, (0, 4)[b], 1, b * HALF, HALF)[:])
+        for b, number in enumerate((0, 4)):
+            nc.scalar.copy(out=y_first[:, halves[b]], in_=down(0, 0, number, 1, b * HALF, HALF)[:])
         place(windows[0], y_first[:], 0, 1)
-        sums = [None] + [down(n, 0, 4 + n) for n in range(1, ROW_TILES)]
-        for n in range(1, 3):
+        sums = {n: down(n, 0, 4 + n) for n in range(1, ROW_TILES)}
+        for n in (1, 2):
             copy_and_place(n, 0, sums[n])
         quantize(1, weave(1, scale(slices_tile(1, "h_first"), act)))
         copy_and_place(3, 0, sums[3], 1, "h_first")
         act = silu(2, up(2, (4, 5), 0))
-        by_slice = scale(slices_tile(2, "planes2"), act, (0, 1))
-        for n in range(3):
+        by_slice = scale(slices_tile(2, "by_slice2"), act, (0, 1))
+        for n in (0, 1, 2):
             copy_and_place(n, 1, down(n, 1, n))
         quantize(2, weave(2, scale(by_slice, act, (2, 3))))
-        copy_and_place(3, 1, down(3, 1, 3), 1, "planes2")
-        by_slice = scale(slices_tile(3, "planes3"), silu(3, up(3, (6, 7), 0)))
+        copy_and_place(3, 1, down(3, 1, 3), 1, "by_slice2")
+        by_slice = scale(slices_tile(3, "by_slice3"), silu(3, up(3, (6, 7), 0)))
         copy_and_place(0, 2, down(0, 2, 0))
         quantize(3, weave(3, by_slice))
-        copy_and_place(1, 2, down(1, 2, 1), 1, "planes3")
-        for n in range(2):
+        copy_and_place(1, 2, down(1, 2, 1), 1, "by_slice3")
+        for n in (0, 1):
             copy_and_place(n, 3, down(n, 3, 2 + n))
-            store(n, windows[n])
-        for n in range(2, 4):
+            store(n)
+        for n in (2, 3):
             copy_and_place(n, 2, down(n, 2, 2 + n, 2), 2)
-            store(n, windows[n])
+            store(n)

@@ -59,14 +59,14 @@ def tile_list_modp_silu_none_kernel(
         h_rest = sbuf("h_rest", [P, J - CHUNK], U32)
         h_s = sbuf("h_s", [P, J], U8)
         windows = [sbuf("window%d" % n, [P, T], F32) for n in range(ON_VECTOR)]
-        sm_at = WORD * T
-        wd_s_at = sm_at + ALIGN
-        wu_raw0 = spanning(after_words, "wu_raw0", R, sm_at - WORD * R, wd_s_at + ALIGN)
+        wu_raw0 = placed(after_words, "wu_raw0", R, I32, 0)[:]
         wu_raw1_at = WORD * T
         tab1_at = wu_raw1_at + WORD * R
         zeros = spanning(after_zeros, "zeros", R // WORD, wu_raw1_at - ALIGN, tab1_at + ALIGN)
-        wgo_at = 2 * N
-        wu_s_raw = spanning(after_scales, "wu_s_raw", R // WORD, 0, wgo_at + ALIGN)
+        wd_s_at = WORD * T
+        wd_at = wd_s_at + N
+        wgo_at = wd_at + 2 * N
+        wu_s_raw = spanning(after_scales, "wu_s_raw", R // WORD, wd_s_at - ALIGN, wgo_at + ALIGN)
 
         nc.vector.memset(tab_s[:], 0)
         nc.vector.memset(zeros, 0)
@@ -198,15 +198,8 @@ def tile_list_modp_silu_none_kernel(
                 out=wu_w[:, a, :].bitcast(U32).rearrange("p (t m i) -> p m t i", t=PACK, i=LINE),
                 in_=wu_raw[a].bitcast(U32).rearrange("p (m i t) -> p m t i", t=PACK, i=LINE),
             )
-        sm_t = placed(after_words, "sm_t", PACK, F32, sm_at)
-        wd_s = placed(after_words, "wd_s", N // WORD, I32, wd_s_at)
+        sm_t = placed(after_words, "sm_t", PACK, F32, 0)
         nc.sync.dma_start(out=sm_t[:], in_=sm.rearrange("(p t) -> p t", t=PACK))
-        windows.append(placed(after_words, "last_window", T, F32, 0))
-        for c0 in range(0, T, T // 4):
-            nc.gpsimd.memset(windows[ON_VECTOR][:, c0 : c0 + T // 4], 0.0)
-        nc.gpsimd.memset(wd_s[:], 0)
-        for q in range(QUADRANTS):
-            nc.sync.dma_start(out=wd_s[32 * q : 32 * q + 4, :], in_=wd_scales[0, 4 * q : 4 * q + 4, :].bitcast(I32))
 
         v_s = sbuf("v_s", [P, J], U8)
         nc.vector.tensor_copy(v_s[:], tab_s[:].bitcast(U8).indirect(offsets[:]))
@@ -217,9 +210,15 @@ def tile_list_modp_silu_none_kernel(
             in_=wu_s_raw.bitcast(U8).rearrange("p (m t) -> p t m", t=PACK),
         )
         gather_chunks(0, 2, 2, placed(after_zeros, "v_w0_2", 2 * CHUNK, U32, wu_raw1_at))
-        wd_w = placed(after_scales, "wd_w", wgo_at // WORD, I32, 0)
+        wd_s = placed(after_scales, "wd_s", N // WORD, I32, wd_s_at)
+        wd_w = placed(after_scales, "wd_w", N // 2, I32, wd_at)
         wgo_t = placed(after_scales, "wgo_t", J, F32, wgo_at)
+        nc.gpsimd.memset(wd_s[:], 0)
+        windows.append(placed(after_scales, "last_window", T, F32, 0))
+        nc.gpsimd.memset(windows[ON_VECTOR][:], 0.0)
         nc.sync.dma_start(out=wd_w[:], in_=wd_words[0].bitcast(I32))
+        for q in range(QUADRANTS):
+            nc.sync.dma_start(out=wd_s[32 * q : 32 * q + 4, :], in_=wd_scales[0, 4 * q : 4 * q + 4, :].bitcast(I32))
         nc.sync.dma_start(out=wgo_t[:], in_=wgo)
         halves = [slice(b * HALF, (b + 1) * HALF) for b in range(2)]
         closing_words = [gather_words(1, halves[b], sbuf("v_half%d" % b, [P, HALF], U32)) for b in range(2)]

@@ -26,6 +26,7 @@ ROW_TILES = N // P
 ON_VECTOR = 3
 LIST_ROWS = 16
 QUADRANTS = 4
+UPPER_FIRST = (2, 3, 0, 1)
 WORD = 4
 LINE = 4
 ALIGN = 64
@@ -79,7 +80,7 @@ def tile_list_modp_silu_none_kernel(
             nc.sync.dma_start(out=tile, in_=words.rearrange("p c i -> p (c i)").bitcast(I32))
 
         def load_scales(tile, scales):
-            for q in range(QUADRANTS):
+            for q in UPPER_FIRST:
                 nc.sync.dma_start(
                     out=tile[32 * q : 32 * q + 4 * PASSES, :], in_=scales[:, 4 * q : 4 * q + 4, :].bitcast(I32)
                 )

@@ -268,10 +268,7 @@ def tile_list_modp_silu_none_kernel(
         by_slice = scale(slices_tile(3, "by_slice3"), silu(3, up(3, (6, 7), 0)))
         copy_and_place(0, 2, down(0, 2, 0))
         quantize(3, weave(3, by_slice))
-        copy_and_place(1, 2, down(1, 2, 1), 1, "by_slice3")
-        for n in (0, 1):
-            copy_and_place(n, 3, down(n, 3, 2 + n))
-            store(n)
-        for n in (2, 3):
-            copy_and_place(n, 2, down(n, 2, 2 + n, 2), 2)
+        copy_and_place(2, 2, down(2, 2, 1), 1, "by_slice3")
+        for n, c, number in ((0, 3, 2), (1, 2, 3), (2, 3, 4), (3, 2, 5)):
+            copy_and_place(n, c, down(n, c, number, 4 - c), 4 - c)
             store(n)

from contextlib import ExitStack

import concourse.mybir as mybir

K, R, N, T, J = 1024, 512, 512, 2048, 1024
FLOPS = 2 * K * R * J + 2 * R * N * J

F32 = mybir.dt.float32
BF16 = mybir.dt.bfloat16
I32 = mybir.dt.int32
U32 = mybir.dt.uint32
U16 = mybir.dt.uint16
U8 = mybir.dt.uint8
FP8X4 = mybir.dt.float8_e4m3fn_x4
FP4X4 = mybir.dt.float4_e2m1fn_x4
ACT = mybir.ActivationFunctionType
MULT = mybir.AluOpType.mult

P = 128
PACK = 4
PASSES = K // (P * PACK)
CHUNK = 256
HALF = CHUNK // 2
QUARTER = CHUNK // 4
ROW_TILES = N // P
ON_VECTOR = 3
LIST_ROWS = 16
QUADRANTS = 4
UPPER_FIRST = (2, 3, 0, 1)
WORD = 4
LINE = 4
ALIGN = 64


def tile_list_modp_silu_none_kernel(
    tc, tab_words, tab_scales, wu_words, wu_scales, sm, wd_words, wd_scales, wgo, offs, out
):
    nc = tc.nc
    with ExitStack() as ctx:
        keep = ctx.enter_context(tc.tile_pool(name="keep", bufs=1))
        after_zeros = ctx.enter_context(tc.tile_pool(name="after_zeros", bufs=1))
        after_scales = ctx.enter_context(tc.tile_pool(name="after_scales", bufs=1))
        after_words = ctx.enter_context(tc.tile_pool(name="after_words", bufs=1))
        psum = ctx.enter_context(tc.psum_pool(name="psum", bufs=1))

        def sbuf(name, shape, dtype, tag=None):
            return keep.tile(shape, dtype, name=name, tag=tag or name, align_bytes=ALIGN)

        def placed(pool, name, columns, dtype, at):
            return pool.tile([P, columns], dtype, name=name, offset=at, align_bytes=ALIGN)

        def spanning(pool, name, columns, start, stop):
            return placed(pool, name, (stop - start) // WORD, I32, start)[:, :columns]

        offsets = keep.tile([P, J // LIST_ROWS], U16, name="offsets")
        tab_s = sbuf("tab_s", [P, T // WORD], I32)
        wu_w = sbuf("wu_w", [P, PASSES, R], I32)
        wu_s = sbuf("wu_s", [P, R], U8)
        h_first = sbuf("h_first", [P, CHUNK], U32)
        h_rest = sbuf("h_rest", [P, J - CHUNK], U32)
        h_s = sbuf("h_s", [P, J], U8)
        windows = [sbuf("window%d" % n, [P, T], F32) for n in range(ON_VECTOR)]
        wu_raw0 = placed(after_words, "wu_raw0", R, I32, 0)[:]
        wu_raw1_at = WORD * T
        tab1_at = wu_raw1_at + WORD * R
        zeros = spanning(after_zeros, "zeros", R // WORD, wu_raw1_at - ALIGN, tab1_at + ALIGN)
        wd_s_at = WORD * T
        wd_at = wd_s_at + N
        wgo_at = wd_at + 2 * N
        wu_s_raw = spanning(after_scales, "wu_s_raw", R // WORD, wd_s_at - ALIGN, wgo_at + ALIGN)

        nc.vector.memset(tab_s[:], 0)
        nc.vector.memset(zeros, 0)
        nc.vector.tensor_copy(wu_s_raw, zeros)

        tab_w = [placed(after_zeros, "tab_w%d" % a, T, I32, at) for a, at in enumerate((0, tab1_at))]
        wu_raw = [wu_raw0, placed(after_zeros, "wu_raw1", R, I32, wu_raw1_at)[:]]

        def load_words(tile, words):
            nc.sync.dma_start(out=tile, in_=words.rearrange("p c i -> p (c i)").bitcast(I32))

        def load_scales(tile, scales):
            for q in UPPER_FIRST:
                nc.sync.dma_start(
                    out=tile[32 * q : 32 * q + 4 * PASSES, :], in_=scales[:, 4 * q : 4 * q + 4, :].bitcast(I32)
                )

        load_words(wu_raw[0], wu_words[0])
        nc.sync.dma_start(offsets[:], offs)
        load_scales(tab_s, tab_scales)
        load_words(tab_w[0][:], tab_words[0])
        load_scales(wu_s_raw, wu_scales)
        load_words(wu_raw[1], wu_words[1])
        load_words(tab_w[1][:], tab_words[1])

        def cols(c, count=1):
            return slice(c * CHUNK, (c + count) * CHUNK)

        def listed(entries):
            return offsets[:, entries.start // LIST_ROWS : entries.stop // LIST_ROWS]

        def gather_words(a, entries, tile):
            nc.vector.tensor_copy(tile[:], tab_w[a][:].bitcast(U32).indirect(listed(entries)))
            return tile[:]

        v_w = {}

        def gather_chunks(a, c, count=1, tile=None):
            if tile is None:
                tile = sbuf("v_w%d_%d" % (a, c), [P, count * CHUNK], U32)
            words = gather_words(a, cols(c, count), tile)
            for i in range(count):
                v_w[a, c + i] = words[:, cols(i)]

        def up_pass(a, bank, slices, words, entries, opening):
            for i, t in enumerate(slices):
                nc.tensor.matmul_mx(
                    out=bank[:, i, :],
                    lhsT=wu_w[:, a, t * P : (t + 1) * P].bitcast(FP8X4),
                    lhsT_scale=wu_s[4 * a :, t * P : (t + 1) * P],
                    rhs=words.bitcast(FP8X4),
                    rhs_scale=v_s[4 * a :, entries],
                    start=(opening and i == 0),
                    stop=(not opening and i == len(slices) - 1),
                )

        def up_banks(shape, numbers):
            return [psum.tile(shape, F32, name="up", tag="bank%d" % b) for b in numbers]

        def up(c, numbers, opening_pass):
            banks = up_banks([P, 2, CHUNK], numbers)
            for a in (opening_pass, 1 - opening_pass):
                for b in range(2):
                    up_pass(a, banks[b], (2 * b, 2 * b + 1), v_w[a, c], cols(c), a == opening_pass)
            return banks

        def silu(c, banks):
            act = sbuf("act%d" % c, [P, PACK, CHUNK], F32, "act")
            for b in range(2):
                nc.scalar.activation(out=act[:, 2 * b : 2 * b + 2, :], in_=banks[b][:], func=ACT.Silu)
            return act

        def slices_tile(c, tag):
            return sbuf("by_slice%d" % c, [P, PACK, CHUNK], BF16, tag)

        def scale(by_slice, act, slices=range(PACK)):
            for t in slices:
                nc.scalar.activation(out=by_slice[:, t, :], in_=act[:, t, :], func=ACT.Copy, scale=sm_t[:, t : t + 1])
            return by_slice

        def weave(c, by_slice):
            h = sbuf("h%d" % c, [P, CHUNK, PACK], BF16)
            nc.scalar.copy(
                out=h[:].rearrange("p (c i) t -> p c t i", i=LINE),
                in_=by_slice[:].rearrange("p t (c i) -> p c t i", i=LINE),
            )
            return h

        def h_words(c, count=1):
            return h_first[:] if c == 0 else h_rest[:, cols(c - 1, count)]

        def quantize(c, h):
            nc.vector.quantize_mx(
                out=h_words(c).bitcast(FP8X4), scales=h_s[:, cols(c)], in_=h[:].rearrange("p j t -> p (j t)")
            )

        def down(n, c, number, count=1, j0=0, width=None):
            width = width or count * CHUNK
            bank = psum.tile([P, width], F32, name="down", tag="bank%d" % number)
            nc.tensor.matmul_mx(
                out=bank[:],
                lhsT=wd_w[:, n * P // 2 : (n + 1) * P // 2].bitcast(U8).bitcast(FP4X4),
                lhsT_scale=wd_s[:].bitcast(U8)[:, n * P : (n + 1) * P],
                rhs=h_words(c, count)[:, j0 : j0 + width].bitcast(FP8X4),
                rhs_scale=h_s[:, c * CHUNK + j0 : c * CHUNK + j0 + width],
                start=True,
                stop=True,
            )
            return bank

        def place(window, y, c, count):
            entries = cols(c, count)
            nc.vector.tensor_tensor(window[:].indirect(listed(entries)), y, wgo_t[:, entries], MULT)

        def copy_and_place(n, c, bank, count=1, tag=None):
            y = sbuf("y%d_%d" % (n, c), [P, count * CHUNK], F32, tag)
            nc.scalar.copy(out=y[:], in_=bank[:])
            place(windows[n], y[:], c, count)

        def store(n):
            nc.sync.dma_start(out=out[n * P : (n + 1) * P, :], in_=windows[n][:])

        for window in windows:
            for c0 in range(0, T, T // 2):
                nc.vector.memset(window[:, c0 : c0 + T // 2], 0.0)

        for a in range(PASSES):
            nc.scalar.copy(
                out=wu_w[:, a, :].bitcast(U32).rearrange("p (t m i) -> p m t i", t=PACK, i=LINE),
                in_=wu_raw[a].bitcast(U32).rearrange("p (m i t) -> p m t i", t=PACK, i=LINE),
            )
        sm_t = placed(after_words, "sm_t", PACK, F32, 0)
        nc.sync.dma_start(out=sm_t[:], in_=sm.rearrange("(p t) -> p t", t=PACK))

        v_s = sbuf("v_s", [P, J], U8)
        nc.vector.tensor_copy(v_s[:], tab_s[:].bitcast(U8).indirect(offsets[:]))
        gather_chunks(0, 0)
        gather_chunks(0, 1)
        nc.vector.tensor_copy(
            out=wu_s[:].rearrange("p (t m) -> p t m", t=PACK),
            in_=wu_s_raw.bitcast(U8).rearrange("p (m t) -> p t m", t=PACK),
        )
        gather_chunks(0, 2, 2, placed(after_zeros, "v_w0_2", 2 * CHUNK, U32, wu_raw1_at))
        wd_s = placed(after_scales, "wd_s", N // WORD, I32, wd_s_at)
        wd_w = placed(after_scales, "wd_w", N // 2, I32, wd_at)
        wgo_t = placed(after_scales, "wgo_t", J, F32, wgo_at)
        nc.gpsimd.memset(wd_s[:], 0)
        windows.append(placed(after_scales, "last_window", T, F32, 0))
        nc.gpsimd.memset(windows[ON_VECTOR][:], 0.0)
        nc.sync.dma_start(out=wd_w[:], in_=wd_words[0].bitcast(I32))
        for q in range(QUADRANTS):
            nc.sync.dma_start(out=wd_s[32 * q : 32 * q + 4, :], in_=wd_scales[0, 4 * q : 4 * q + 4, :].bitcast(I32))
        nc.sync.dma_start(out=wgo_t[:], in_=wgo)
        halves = [slice(b * HALF, (b + 1) * HALF) for b in range(2)]
        closing_words = [gather_words(1, halves[b], sbuf("v_half%d" % b, [P, HALF], U32)) for b in range(2)]
        gather_chunks(1, 1)
        gather_chunks(1, 2)

        first = up_banks([P, PACK, HALF], (0, 1))
        for b in range(2):
            up_pass(0, first[b], range(PACK), v_w[0, 0][:, halves[b]], halves[b], True)
        h_halves = []
        for b in range(2):
            up_pass(1, first[b], range(PACK), closing_words[b], halves[b], False)
            h_half = sbuf("h0_%d" % b, [P, HALF, PACK], BF16)[:]
            for q in range(2):
                part = slice(q * QUARTER, (q + 1) * QUARTER)
                act = sbuf("act0_%d" % (2 * b + q), [P, QUARTER, PACK], F32)
                nc.scalar.activation(out=act[:], in_=first[b][:, :, part].rearrange("p t j -> p j t"), func=ACT.Silu)
                nc.vector.tensor_tensor(
                    h_half[:, part, :], act[:], sm_t[:].unsqueeze(1).to_broadcast([P, QUARTER, PACK]), MULT
                )
            h_halves.append(h_half)
        for b in range(2):
            nc.vector.quantize_mx(
                out=h_first[:, halves[b]].bitcast(FP8X4),
                scales=h_s[:, halves[b]],
                in_=h_halves[b].rearrange("p j t -> p (j t)"),
            )
        gather_chunks(1, 3, 1, sbuf("v_w1_3", [P, CHUNK], U32, "act0_3"))

        act = silu(1, up(1, (2, 3), 1))
        y_first = sbuf("y_first", [P, CHUNK], F32)
        for b, number in enumerate((0, 4)):
            nc.scalar.copy(out=y_first[:, halves[b]], in_=down(0, 0, number, 1, b * HALF, HALF)[:])
        place(windows[0], y_first[:], 0, 1)
        sums = {n: down(n, 0, 4 + n) for n in range(1, ROW_TILES)}
        for n in (1, 2):
            copy_and_place(n, 0, sums[n])
        quantize(1, weave(1, scale(slices_tile(1, "h_first"), act)))
        copy_and_place(3, 0, sums[3], 1, "h_first")
        act = silu(2, up(2, (4, 5), 0))
        by_slice = scale(slices_tile(2, "by_slice2"), act, (0, 1))
        for n in (0, 1, 2):
            copy_and_place(n, 1, down(n, 1, n))
        quantize(2, weave(2, scale(by_slice, act, (2, 3))))
        copy_and_place(3, 1, down(3, 1, 3), 1, "by_slice2")
        by_slice = scale(slices_tile(3, "by_slice3"), silu(3, up(3, (6, 7), 0)))
        copy_and_place(0, 2, down(0, 2, 0))
        quantize(3, weave(3, by_slice))
        copy_and_place(2, 2, down(2, 2, 1), 1, "by_slice3")
        for n, c, number in ((0, 3, 2), (1, 2, 3), (2, 3, 4), (3, 2, 5)):
            copy_and_place(n, c, down(n, c, number, 4 - c), 4 - c)
            store(n)
